import numpy as np
import ml_dtypes


def mxq(x, axis, fmt="e4m3"):
    dtype, down = {"e4m3": (ml_dtypes.float8_e4m3fn, 7), "e5m2": (ml_dtypes.float8_e5m2, 14)}[fmt]
    v = np.moveaxis(np.asarray(x, np.float32).astype(ml_dtypes.bfloat16).astype(np.float64), axis, -1)
    blocks = v.reshape(v.shape[:-1] + (-1, 32))
    amax = np.abs(blocks).max(-1, keepdims=True)
    byte = np.maximum(np.where(amax > 0, np.frexp(amax)[1] - 1 + 127, 0) - down, 1)
    scale = np.exp2(byte - 127.0)
    codes = (blocks / scale).astype(np.float32).astype(dtype).astype(np.float64)
    return np.moveaxis((codes * scale).reshape(v.shape), -1, axis)


WIDE = False


def mx_kscale(k):
    if not WIDE:
        return np.ones(k)
    levels = np.array([10, -10, 5, -5, 0])
    if k % 512:
        return np.exp2(np.random.permutation(np.resize(levels, k // 32))).repeat(32)
    a = np.empty((k // 512, 16))
    for p in range(k // 512):
        a[p, :8] = np.random.permutation(np.resize(levels, 8))
        for g in range(8):
            far = levels[np.abs(levels - a[p, g]) >= 10]
            a[p, g + 8] = far[np.random.randint(len(far))]
    return np.exp2(a.ravel()).repeat(32)


def f64(x):
    return np.asarray(x).astype(np.float64)


def striped(idx):
    return np.tile(idx.reshape(-1, 16).T, (8, 1)).astype(np.uint16)


def unstriped(offs):
    return offs[:16].T.reshape(-1).astype(np.int64)


def striped8(idx):
    return np.concatenate([x.reshape(-1, 16).T for x in idx]).astype(np.uint16)


def runs(offs, k):
    lists = np.stack([offs[16 * r : 16 * r + 16].T.reshape(-1) for r in range(8)]).astype(np.int64)
    return lists[np.arange(k) % 512 // 64]


def pack_weight(w):
    k, n = w.shape
    w = f64(np.asarray(w, np.float32).astype(ml_dtypes.bfloat16)).reshape(k // 32, 32, n)
    amax = np.abs(w).max(1)
    byte = np.clip(np.where(amax > 0, np.frexp(amax)[1] - 1 + 127 - 7, 1), 1, 254)
    scaled = (w * np.exp2(127.0 - byte)[:, None, :]).reshape(k, n).astype(np.float32)
    words = np.ascontiguousarray(scaled.reshape(k // 512, 128, 4, n).transpose(0, 1, 3, 2)).astype(ml_dtypes.float8_e4m3fn).view(np.uint8)
    return words, np.ascontiguousarray(byte.astype(np.uint8).reshape(k // 512, 16, n))


def unpack_weight(words, scales):
    g, p, n, _ = words.shape
    vals = np.ascontiguousarray(words).view(ml_dtypes.float8_e4m3fn).astype(np.float64) * np.repeat(np.exp2(scales.astype(np.float64) - 127.0), 8, axis=1)[..., None]
    return vals.transpose(0, 1, 3, 2).reshape(g * 512, n)


def relu(v):
    return np.maximum(v, 0.0)


K, T, S, V, N, H = 512, 2048, 512, 256, 512, 512


def setup_inputs():
    n = np.random.standard_normal
    s = mx_kscale(K)[:, None]
    u = mx_kscale(S)
    packed_xT = pack_weight(n((K, T)) * s)
    return {
        "x_words": packed_xT[0],
        "x_scales": packed_xT[1],
        "wa": (n((K, H)) / np.sqrt(K) / s).astype(np.float32),
        "gt": (np.random.uniform(0.5, 1.5, (S, 1)) * u[:, None]).astype(np.float32),
        "w1": (n((S, N)) / np.sqrt(S) / u[:, None]).astype(np.float32),
        "offs": striped(np.random.permutation(T)[:S]),
        "fl": striped8(np.stack([np.random.permutation(H)[:V] for _ in range(8)])),
    }


def reference(x_words, x_scales, wa, gt, w1, offs, fl):
    xq = unpack_weight(x_words, x_scales)[:, unstriped(offs)]
    y = xq.T @ mxq(f64(wa), 0, "e4m3")
    z = f64(gt) * (relu(y[np.arange(S)[:, None], runs(fl, S)]))
    return mxq(f64(w1), 0, "e4m3").T @ mxq(z, 0, "e4m3")

@@ -1,0 +1,154 @@
+from contextlib import ExitStack
+
+import concourse.mybir as mybir
+
+K, T, S, V, N, H = 512, 2048, 512, 256, 512, 512
+FLOPS = 2 * K * S * H + 2 * S * N * V
+
+F32 = mybir.dt.float32
+BF16 = mybir.dt.bfloat16
+I32 = mybir.dt.int32
+U32 = mybir.dt.uint32
+U16 = mybir.dt.uint16
+U8 = mybir.dt.uint8
+FP8X4 = mybir.dt.float8_e4m3fn_x4
+ALU = mybir.AluOpType
+ACT = mybir.ActivationFunctionType
+
+P = 128
+PACK = 4
+HALF = 256
+
+
+def interleave(copy, grouped, raw, lo, hi):
+    copy(
+        out=grouped[:, PACK * lo : PACK * hi].rearrange("p (c i t) -> p c t i", i=4, t=PACK),
+        in_=raw[:, :, lo:hi].rearrange("p t (c i) -> p c t i", i=4),
+    )
+
+
+def quantize(nc, codes, scales, grouped, lo, hi):
+    nc.vector.quantize_mx(
+        out=codes[:, lo:hi].bitcast(FP8X4), scales=scales[:, lo:hi], in_=grouped[:, PACK * lo : PACK * hi]
+    )
+
+
+def tile_picked_tokmixl_relu_p_kernel(tc, x_words, x_scales, wa, gt, w1, offs, fl, out):
+    nc = tc.nc
+    with ExitStack() as ctx:
+        keep = ctx.enter_context(tc.tile_pool(name="keep", bufs=1))
+        psum = ctx.enter_context(tc.psum_pool(name="psum", bufs=1))
+
+        offs_sb = keep.tile([P, S // 16], U16, name="offs_sb")
+        fl_sb = keep.tile([P, V // 16], U16, name="fl_sb")
+        table_words = keep.tile([P, T], I32, name="table_words", align_bytes=64)
+        table_scales = keep.tile([P, T], U8, name="table_scales", align_bytes=64)
+        gt_sb = keep.tile([P, PACK], F32, name="gt_sb")
+        wa_raw = [keep.tile([P, PACK, HALF], F32, name=f"wa_raw{h}") for h in range(2)]
+        w1_raw = [keep.tile([P, PACK, HALF], F32, name=f"w1_raw{h}", tag=f"w1_raw{h}", align_bytes=64) for h in range(2)]
+
+        x_rows = x_words[0].rearrange("p n t -> p (n t)").bitcast(I32)
+        wa_rows = wa.rearrange("(p t) c -> p t c", t=PACK)
+        w1_rows = w1.rearrange("(p t) c -> p t c", t=PACK)
+        nc.vector.memset(table_scales[:].bitcast(I32), 0)
+        nc.sync.dma_start(offs_sb[:], offs)
+        nc.scalar.dma_start(gt_sb[:], gt.rearrange("(p t) o -> p (t o)", t=PACK))
+        nc.sync.dma_start(table_words[:, : T // 4], x_rows[:, : T // 4])
+        for q in range(4):
+            queue = nc.sync if q < 2 else nc.scalar
+            queue.dma_start(
+                table_scales[32 * q : 32 * q + 4, :].bitcast(I32), x_scales[0, 4 * q : 4 * q + 4, :].bitcast(I32)
+            )
+        nc.sync.dma_start(table_words[:, T // 4 :], x_rows[:, T // 4 :])
+        for h in range(2):
+            nc.sync.dma_start(wa_raw[h][:], wa_rows[:, :, h * HALF : (h + 1) * HALF])
+        nc.sync.dma_start(fl_sb[:], fl)
+        for h in range(2):
+            nc.sync.dma_start(w1_raw[h][:], w1_rows[:, :, h * HALF : (h + 1) * HALF])
+
+        picked_scales = keep.tile([P, S], U8, name="picked_scales", align_bytes=64)
+        x_sc = keep.tile([P, S], U8, name="x_sc", align_bytes=64)
+        x_codes = keep.tile([P, S], U32, name="x_codes", align_bytes=64)
+        nc.vector.tensor_copy(picked_scales[:], table_scales[:].indirect(offs_sb[:]))
+        nc.vector.tensor_copy(
+            out=x_sc[:].rearrange("p (t m) -> p m t", t=PACK), in_=picked_scales[:].rearrange("p (m t) -> p m t", t=PACK)
+        )
+        nc.vector.tensor_copy(
+            x_codes[:].rearrange("p (t m) -> p m t", t=PACK), table_words[:].bitcast(U32).indirect(offs_sb[:])
+        )
+
+        gt_wide = keep.tile([P, PACK, V], F32, name="gt_wide")
+        nc.scalar.copy(out=gt_wide[:], in_=gt_sb[:].unsqueeze(2).to_broadcast([P, PACK, V]))
+
+        wa_codes = [keep.tile([P, HALF], U32, name=f"wa_codes{h}", align_bytes=64) for h in range(2)]
+        wa_sc = [keep.tile([P, HALF], U8, name=f"wa_sc{h}", align_bytes=64) for h in range(2)]
+        y = [keep.tile([P, H], F32, name=f"y{t}", align_bytes=64) for t in range(PACK)]
+        acc = {}
+
+        def project(h, t):
+            acc[h, t] = psum.tile([P, HALF], F32, name=f"acc{h}{t}", tag=f"bank{bank[h, t]}")
+            nc.tensor.matmul_mx(
+                out=acc[h, t][:],
+                lhsT=x_codes[:, t * P : (t + 1) * P].bitcast(FP8X4),
+                lhsT_scale=x_sc[:, t * P : (t + 1) * P],
+                rhs=wa_codes[h][:].bitcast(FP8X4),
+                rhs_scale=wa_sc[h][:],
+                start=True,
+                stop=True,
+            )
+
+        bank = {(h, t): PACK * h + t for h in range(2) for t in range(PACK)}
+        bank[0, 3] = bank[1, 0]
+        wa_grouped = [keep.tile([P, PACK * HALF], BF16, name=f"wa_grouped{h}", align_bytes=64) for h in range(2)]
+        interleave(nc.scalar.copy, wa_grouped[0], wa_raw[0], 0, P)
+        interleave(nc.vector.tensor_copy, wa_grouped[0], wa_raw[0], P, HALF)
+        quantize(nc, wa_codes[0], wa_sc[0], wa_grouped[0], 0, HALF)
+        for lo in (0, P):
+            interleave(nc.vector.tensor_copy, wa_grouped[1], wa_raw[1], lo, lo + P)
+        for lo in (0, P):
+            quantize(nc, wa_codes[1], wa_sc[1], wa_grouped[1], lo, lo + P)
+
+        w1_grouped = [keep.tile([P, PACK * HALF], BF16, name=f"w1_grouped{h}", align_bytes=64) for h in range(2)]
+        w1_codes = [keep.tile([P, HALF], U32, name=f"w1_codes{h}", align_bytes=64) for h in range(2)]
+        w1_sc = [keep.tile([P, HALF], U8, name=f"w1_sc{h}", align_bytes=64) for h in range(2)]
+        interleave(nc.vector.tensor_copy, w1_grouped[0], w1_raw[0], 0, HALF)
+        nc.vector.quantize_mx(out=w1_codes[0][:].bitcast(FP8X4), scales=w1_sc[0][:], in_=w1_grouped[0][:])
+
+        z = keep.tile([P, PACK, V], F32, name="z", tag="w1_raw0", align_bytes=64)
+        for t in range(PACK):
+            for h in range(2):
+                project(h, t)
+                nc.scalar.activation(out=y[t][:, h * HALF : (h + 1) * HALF], in_=acc[h, t][:], func=ACT.Relu)
+            for lo, hi in ((0, V),) if t < PACK - 1 else ((0, P), (P, V)):
+                nc.vector.tensor_tensor(
+                    z[:, t, lo:hi], y[t][:].indirect(fl_sb[:, lo // 16 : hi // 16]), gt_wide[:, t, lo:hi], ALU.mult
+                )
+        interleave(nc.scalar.copy, w1_grouped[1], w1_raw[1], 0, HALF)
+
+        z_grouped = keep.tile([P, PACK * V], BF16, name="z_grouped", align_bytes=64)
+        z_codes = keep.tile([P, V], U32, name="z_codes", align_bytes=64)
+        z_sc = keep.tile([P, V], U8, name="z_sc", align_bytes=64)
+        for lo in (0, P):
+            interleave(nc.vector.tensor_copy, z_grouped, z, lo, lo + P)
+        for lo in (0, P):
+            quantize(nc, z_codes, z_sc, z_grouped, lo, lo + P)
+        nc.vector.quantize_mx(out=w1_codes[1][:].bitcast(FP8X4), scales=w1_sc[1][:], in_=w1_grouped[1][:])
+
+        for u in range(N // P):
+            cols = slice((u % 2) * P, (u % 2 + 1) * P)
+            total = psum.tile([P, V], F32, name=f"total{u}", tag=f"bank{u}")
+            nc.tensor.matmul_mx(
+                out=total[:],
+                lhsT=w1_codes[u // 2][:, cols].bitcast(FP8X4),
+                lhsT_scale=w1_sc[u // 2][:, cols],
+                rhs=z_codes[:].bitcast(FP8X4),
+                rhs_scale=z_sc[:],
+                start=True,
+                stop=True,
+            )
+            result = keep.tile([P, V], F32, name=f"result{u}")
+            if u % 2 == 0:
+                nc.scalar.copy(out=result[:], in_=total[:])
+            else:
+                nc.vector.tensor_copy(out=result[:], in_=total[:])
+            nc.sync.dma_start(out[u * P : (u + 1) * P, :], result[:])

@@ -22,8 +22,8 @@ HALF = 256
 
 def interleave(copy, grouped, raw, lo, hi):
     copy(
-        out=grouped[:, PACK * lo : PACK * hi].rearrange("p (c i t) -> p c t i", i=4, t=PACK),
-        in_=raw[:, :, lo:hi].rearrange("p t (c i) -> p c t i", i=4),
+        out=grouped[:, PACK * lo : PACK * hi].rearrange("p (c i t) -> p c t i", i=2, t=PACK),
+        in_=raw[:, :, lo:hi].rearrange("p t (c i) -> p c t i", i=2),
     )
 
 
@@ -44,7 +44,7 @@ def tile_picked_tokmixl_relu_p_kernel(tc, x_words, x_scales, wa, gt, w1, offs, f
         table_words = keep.tile([P, T], I32, name="table_words", align_bytes=64)
         table_scales = keep.tile([P, T], U8, name="table_scales", align_bytes=64)
         gt_sb = keep.tile([P, PACK], F32, name="gt_sb")
-        wa_raw = [keep.tile([P, PACK, HALF], F32, name=f"wa_raw{h}") for h in range(2)]
+        wa_raw = keep.tile([P, PACK, H], F32, name="wa_raw", align_bytes=64)
         w1_raw = [keep.tile([P, PACK, HALF], F32, name=f"w1_raw{h}", tag=f"w1_raw{h}", align_bytes=64) for h in range(2)]
 
         x_rows = x_words[0].rearrange("p n t -> p (n t)").bitcast(I32)
@@ -60,8 +60,7 @@ def tile_picked_tokmixl_relu_p_kernel(tc, x_words, x_scales, wa, gt, w1, offs, f
                 table_scales[32 * q : 32 * q + 4, :].bitcast(I32), x_scales[0, 4 * q : 4 * q + 4, :].bitcast(I32)
             )
         nc.sync.dma_start(table_words[:, T // 4 :], x_rows[:, T // 4 :])
-        for h in range(2):
-            nc.sync.dma_start(wa_raw[h][:], wa_rows[:, :, h * HALF : (h + 1) * HALF])
+        nc.sync.dma_start(wa_raw[:], wa_rows)
         nc.sync.dma_start(fl_sb[:], fl)
         for h in range(2):
             nc.sync.dma_start(w1_raw[h][:], w1_rows[:, :, h * HALF : (h + 1) * HALF])
@@ -71,17 +70,37 @@ def tile_picked_tokmixl_relu_p_kernel(tc, x_words, x_scales, wa, gt, w1, offs, f
         x_codes = keep.tile([P, S], U32, name="x_codes", align_bytes=64)
         nc.vector.tensor_copy(picked_scales[:], table_scales[:].indirect(offs_sb[:]))
         nc.vector.tensor_copy(
-            out=x_sc[:].rearrange("p (t m) -> p m t", t=PACK), in_=picked_scales[:].rearrange("p (m t) -> p m t", t=PACK)
+            out=x_sc[:].rearrange("p (t c i) -> p c t i", t=PACK, i=16),
+            in_=picked_scales[:].rearrange("p (c i t) -> p c t i", t=PACK, i=16),
         )
-        nc.vector.tensor_copy(
-            x_codes[:].rearrange("p (t m) -> p m t", t=PACK), table_words[:].bitcast(U32).indirect(offs_sb[:])
-        )
+
+        picked_words = [keep.tile([P, S // 2], U32, name=f"picked_words{g}", align_bytes=64) for g in range(2)]
+        for g in range(2):
+            nc.vector.tensor_copy(
+                picked_words[g][:], table_words[:].bitcast(U32).indirect(offs_sb[:, g * 16 : (g + 1) * 16])
+            )
+        for g in range(2):
+            nc.vector.tensor_copy(
+                out=x_codes[:].bitcast(I32).rearrange("p (t g m) -> p g m t", t=PACK, g=2)[:, g],
+                in_=picked_words[g][:].bitcast(I32).rearrange("p (m t) -> p m t", t=PACK),
+            )
 
         gt_wide = keep.tile([P, PACK, V], F32, name="gt_wide")
         nc.scalar.copy(out=gt_wide[:], in_=gt_sb[:].unsqueeze(2).to_broadcast([P, PACK, V]))
 
-        wa_codes = [keep.tile([P, HALF], U32, name=f"wa_codes{h}", align_bytes=64) for h in range(2)]
-        wa_sc = [keep.tile([P, HALF], U8, name=f"wa_sc{h}", align_bytes=64) for h in range(2)]
+        wa_codes = keep.tile([P, H], U32, name="wa_codes", align_bytes=64)
+        wa_sc = keep.tile([P, H], U8, name="wa_sc", align_bytes=64)
+        wa_grouped = keep.tile([P, PACK * H], BF16, name="wa_grouped", align_bytes=64)
+        interleave(nc.scalar.copy, wa_grouped, wa_raw, 0, 128)
+        interleave(nc.vector.tensor_copy, wa_grouped, wa_raw, 128, 256)
+        interleave(nc.scalar.copy, wa_grouped, wa_raw, 256, 320)
+        interleave(nc.vector.tensor_copy, wa_grouped, wa_raw, 320, H)
+        for lo in (0, HALF):
+            quantize(nc, wa_codes, wa_sc, wa_grouped, lo, lo + HALF)
+
+        bank = {(h, t): PACK * h + t for h in range(2) for t in range(PACK)}
+        bank[0, 2] = bank[1, 0]
+        bank[0, 3] = bank[1, 1]
         y = [keep.tile([P, H], F32, name=f"y{t}", align_bytes=64) for t in range(PACK)]
         acc = {}
 
@@ -91,25 +110,14 @@ def tile_picked_tokmixl_relu_p_kernel(tc, x_words, x_scales, wa, gt, w1, offs, f
                 out=acc[h, t][:],
                 lhsT=x_codes[:, t * P : (t + 1) * P].bitcast(FP8X4),
                 lhsT_scale=x_sc[:, t * P : (t + 1) * P],
-                rhs=wa_codes[h][:].bitcast(FP8X4),
-                rhs_scale=wa_sc[h][:],
+                rhs=wa_codes[:, h * HALF : (h + 1) * HALF].bitcast(FP8X4),
+                rhs_scale=wa_sc[:, h * HALF : (h + 1) * HALF],
                 start=True,
                 stop=True,
             )
 
-        bank = {(h, t): PACK * h + t for h in range(2) for t in range(PACK)}
-        bank[0, 3] = bank[1, 0]
-        wa_grouped = [keep.tile([P, PACK * HALF], BF16, name=f"wa_grouped{h}", align_bytes=64) for h in range(2)]
-        interleave(nc.scalar.copy, wa_grouped[0], wa_raw[0], 0, P)
-        interleave(nc.vector.tensor_copy, wa_grouped[0], wa_raw[0], P, HALF)
-        quantize(nc, wa_codes[0], wa_sc[0], wa_grouped[0], 0, HALF)
-        for lo in (0, P):
-            interleave(nc.vector.tensor_copy, wa_grouped[1], wa_raw[1], lo, lo + P)
-        for lo in (0, P):
-            quantize(nc, wa_codes[1], wa_sc[1], wa_grouped[1], lo, lo + P)
-
         w1_grouped = [keep.tile([P, PACK * HALF], BF16, name=f"w1_grouped{h}", align_bytes=64) for h in range(2)]
-        w1_codes = [keep.tile([P, HALF], U32, name=f"w1_codes{h}", align_bytes=64) for h in range(2)]
+        w1_codes = [keep.tile([P, HALF], U32, name="w1_codes0", align_bytes=64)]
         w1_sc = [keep.tile([P, HALF], U8, name=f"w1_sc{h}", align_bytes=64) for h in range(2)]
         interleave(nc.vector.tensor_copy, w1_grouped[0], w1_raw[0], 0, HALF)
         nc.vector.quantize_mx(out=w1_codes[0][:].bitcast(FP8X4), scales=w1_sc[0][:], in_=w1_grouped[0][:])
@@ -125,13 +133,14 @@ def tile_picked_tokmixl_relu_p_kernel(tc, x_words, x_scales, wa, gt, w1, offs, f
                 )
         interleave(nc.scalar.copy, w1_grouped[1], w1_raw[1], 0, HALF)
 
-        z_grouped = keep.tile([P, PACK * V], BF16, name="z_grouped", align_bytes=64)
+        z_grouped = keep.tile([P, PACK * V], BF16, name="z_grouped", tag="z_grouped", align_bytes=64)
         z_codes = keep.tile([P, V], U32, name="z_codes", align_bytes=64)
         z_sc = keep.tile([P, V], U8, name="z_sc", align_bytes=64)
         for lo in (0, P):
             interleave(nc.vector.tensor_copy, z_grouped, z, lo, lo + P)
         for lo in (0, P):
             quantize(nc, z_codes, z_sc, z_grouped, lo, lo + P)
+        w1_codes.append(keep.tile([P, HALF], U32, name="w1_codes1", tag="z_grouped", align_bytes=64))
         nc.vector.quantize_mx(out=w1_codes[1][:].bitcast(FP8X4), scales=w1_sc[1][:], in_=w1_grouped[1][:])
 
         for u in range(N // P):

@@ -51,9 +51,9 @@ def tile_picked_tokmixl_relu_p_kernel(tc, x_words, x_scales, wa, gt, w1, offs, f
         wa_rows = wa.rearrange("(p t) c -> p t c", t=PACK)
         w1_rows = w1.rearrange("(p t) c -> p t c", t=PACK)
         nc.vector.memset(table_scales[:].bitcast(I32), 0)
+        nc.sync.dma_start(table_words[:, : T // 4], x_rows[:, : T // 4])
         nc.sync.dma_start(offs_sb[:], offs)
         nc.scalar.dma_start(gt_sb[:], gt.rearrange("(p t) o -> p (t o)", t=PACK))
-        nc.sync.dma_start(table_words[:, : T // 4], x_rows[:, : T // 4])
         for q in range(4):
             queue = nc.sync if q < 2 else nc.scalar
             queue.dma_start(
@@ -85,8 +85,8 @@ def tile_picked_tokmixl_relu_p_kernel(tc, x_words, x_scales, wa, gt, w1, offs, f
                 in_=picked_words[g][:].bitcast(I32).rearrange("p (m t) -> p m t", t=PACK),
             )
 
-        gt_wide = keep.tile([P, PACK, V], F32, name="gt_wide")
-        nc.scalar.copy(out=gt_wide[:], in_=gt_sb[:].unsqueeze(2).to_broadcast([P, PACK, V]))
+        gt_wide = keep.tile([P, 2, V], F32, name="gt_wide")
+        nc.scalar.copy(out=gt_wide[:], in_=gt_sb[:, 2:].unsqueeze(2).to_broadcast([P, 2, V]))
 
         wa_codes = keep.tile([P, H], U32, name="wa_codes", align_bytes=64)
         wa_sc = keep.tile([P, H], U8, name="wa_sc", align_bytes=64)
@@ -116,21 +116,28 @@ def tile_picked_tokmixl_relu_p_kernel(tc, x_words, x_scales, wa, gt, w1, offs, f
                 stop=True,
             )
 
-        w1_grouped = [keep.tile([P, PACK * HALF], BF16, name=f"w1_grouped{h}", align_bytes=64) for h in range(2)]
+        w1_grouped = [keep.tile([P, PACK * HALF], BF16, name="w1_grouped0", align_bytes=64)]
         w1_codes = [keep.tile([P, HALF], U32, name="w1_codes0", align_bytes=64)]
         w1_sc = [keep.tile([P, HALF], U8, name=f"w1_sc{h}", align_bytes=64) for h in range(2)]
         interleave(nc.vector.tensor_copy, w1_grouped[0], w1_raw[0], 0, HALF)
         nc.vector.quantize_mx(out=w1_codes[0][:].bitcast(FP8X4), scales=w1_sc[0][:], in_=w1_grouped[0][:])
 
-        z = keep.tile([P, PACK, V], F32, name="z", tag="w1_raw0", align_bytes=64)
+        looked_up = keep.tile([P, 2, V], F32, name="looked_up", tag="w1_raw0", align_bytes=64)
+        z = keep.tile([P, PACK, V], F32, name="z", align_bytes=64)
         for t in range(PACK):
             for h in range(2):
                 project(h, t)
                 nc.scalar.activation(out=y[t][:, h * HALF : (h + 1) * HALF], in_=acc[h, t][:], func=ACT.Relu)
-            for lo, hi in ((0, V),) if t < PACK - 1 else ((0, P), (P, V)):
-                nc.vector.tensor_tensor(
-                    z[:, t, lo:hi], y[t][:].indirect(fl_sb[:, lo // 16 : hi // 16]), gt_wide[:, t, lo:hi], ALU.mult
-                )
+            if t < 2:
+                nc.vector.tensor_copy(looked_up[:, t, :], y[t][:].indirect(fl_sb[:]))
+            else:
+                for lo, hi in ((0, V),) if t < PACK - 1 else ((0, P), (P, V)):
+                    nc.vector.tensor_tensor(
+                        z[:, t, lo:hi], y[t][:].indirect(fl_sb[:, lo // 16 : hi // 16]), gt_wide[:, t - 2, lo:hi], ALU.mult
+                    )
+        for t in range(2):
+            nc.scalar.activation(out=z[:, t, :], in_=looked_up[:, t, :], func=ACT.Copy, scale=gt_sb[:, t : t + 1])
+        w1_grouped.append(keep.tile([P, PACK * HALF], BF16, name="w1_grouped1", tag="w1_raw0", align_bytes=64))
         interleave(nc.scalar.copy, w1_grouped[1], w1_raw[1], 0, HALF)
 
         z_grouped = keep.tile([P, PACK * V], BF16, name="z_grouped", tag="z_grouped", align_bytes=64)
@@ -141,23 +148,24 @@ def tile_picked_tokmixl_relu_p_kernel(tc, x_words, x_scales, wa, gt, w1, offs, f
         for lo in (0, P):
             quantize(nc, z_codes, z_sc, z_grouped, lo, lo + P)
         w1_codes.append(keep.tile([P, HALF], U32, name="w1_codes1", tag="z_grouped", align_bytes=64))
-        nc.vector.quantize_mx(out=w1_codes[1][:].bitcast(FP8X4), scales=w1_sc[1][:], in_=w1_grouped[1][:])
+        for lo in (0, P):
+            quantize(nc, w1_codes[1], w1_sc[1], w1_grouped[1], lo, lo + P)
 
-        for u in range(N // P):
+        total = [psum.tile([P, V], F32, name=f"total{u}", tag=f"bank{u}") for u in range(N // P)]
+        pieces = [(u, lo, lo + P) for lo in (0, P) for u in range(2)] + [(u, 0, V) for u in range(2, N // P)]
+        for u, lo, hi in pieces:
             cols = slice((u % 2) * P, (u % 2 + 1) * P)
-            total = psum.tile([P, V], F32, name=f"total{u}", tag=f"bank{u}")
             nc.tensor.matmul_mx(
-                out=total[:],
+                out=total[u][:, lo:hi],
                 lhsT=w1_codes[u // 2][:, cols].bitcast(FP8X4),
                 lhsT_scale=w1_sc[u // 2][:, cols],
-                rhs=z_codes[:].bitcast(FP8X4),
-                rhs_scale=z_sc[:],
+                rhs=z_codes[:, lo:hi].bitcast(FP8X4),
+                rhs_scale=z_sc[:, lo:hi],
                 start=True,
                 stop=True,
             )
+        for u in range(N // P):
             result = keep.tile([P, V], F32, name=f"result{u}")
-            if u % 2 == 0:
-                nc.scalar.copy(out=result[:], in_=total[:])
-            else:
-                nc.vector.tensor_copy(out=result[:], in_=total[:])
+            copy = nc.vector.tensor_copy if u % 2 else nc.scalar.copy
+            copy(out=result[:], in_=total[u][:])
             nc.sync.dma_start(out[u * P : (u + 1) * P, :], result[:])

@@ -20,10 +20,14 @@ PACK = 4
 HALF = 256
 
 
-def interleave(copy, grouped, raw, lo, hi):
+RUN = 4
+X_FIRST = T // 4
+
+
+def interleave(copy, grouped, raw, lo, hi, at=0):
     copy(
-        out=grouped[:, PACK * lo : PACK * hi].rearrange("p (c i t) -> p c t i", i=2, t=PACK),
-        in_=raw[:, :, lo:hi].rearrange("p t (c i) -> p c t i", i=2),
+        out=grouped[:, PACK * (at + lo) : PACK * (at + hi)].rearrange("p (c i t) -> p c t i", i=RUN, t=PACK),
+        in_=raw[:, :, lo:hi].rearrange("p t (c i) -> p c t i", i=RUN),
     )
 
 
@@ -37,6 +41,7 @@ def tile_picked_tokmixl_relu_p_kernel(tc, x_words, x_scales, wa, gt, w1, offs, f
     nc = tc.nc
     with ExitStack() as ctx:
         keep = ctx.enter_context(tc.tile_pool(name="keep", bufs=1))
+        shared = ctx.enter_context(tc.tile_pool(name="shared", bufs=1))
         psum = ctx.enter_context(tc.psum_pool(name="psum", bufs=1))
 
         offs_sb = keep.tile([P, S // 16], U16, name="offs_sb")
@@ -44,14 +49,21 @@ def tile_picked_tokmixl_relu_p_kernel(tc, x_words, x_scales, wa, gt, w1, offs, f
         table_words = keep.tile([P, T], I32, name="table_words", align_bytes=64)
         table_scales = keep.tile([P, T], U8, name="table_scales", align_bytes=64)
         gt_sb = keep.tile([P, PACK], F32, name="gt_sb")
-        wa_raw = keep.tile([P, PACK, H], F32, name="wa_raw", align_bytes=64)
-        w1_raw = [keep.tile([P, PACK, HALF], F32, name=f"w1_raw{h}", tag=f"w1_raw{h}", align_bytes=64) for h in range(2)]
+        wa_raw = [
+            keep.tile([P, PACK, HALF], F32, name="wa_raw0", align_bytes=64),
+            shared.tile([P, PACK, P], F32, name="wa_raw1", align_bytes=64, offset=0),
+            keep.tile([P, PACK, P], F32, name="wa_raw2", align_bytes=64),
+        ]
+        w1_raw = [
+            keep.tile([P, PACK, HALF], F32, name="w1_raw0", align_bytes=64),
+            keep.tile([P, PACK, HALF], F32, name="w1_raw1", tag="w1_raw1", align_bytes=64),
+        ]
 
         x_rows = x_words[0].rearrange("p n t -> p (n t)").bitcast(I32)
         wa_rows = wa.rearrange("(p t) c -> p t c", t=PACK)
         w1_rows = w1.rearrange("(p t) c -> p t c", t=PACK)
         nc.vector.memset(table_scales[:].bitcast(I32), 0)
-        nc.sync.dma_start(table_words[:, : T // 4], x_rows[:, : T // 4])
+        nc.sync.dma_start(table_words[:, : X_FIRST], x_rows[:, : X_FIRST])
         nc.sync.dma_start(offs_sb[:], offs)
         nc.scalar.dma_start(gt_sb[:], gt.rearrange("(p t) o -> p (t o)", t=PACK))
         for q in range(4):
@@ -59,9 +71,11 @@ def tile_picked_tokmixl_relu_p_kernel(tc, x_words, x_scales, wa, gt, w1, offs, f
             queue.dma_start(
                 table_scales[32 * q : 32 * q + 4, :].bitcast(I32), x_scales[0, 4 * q : 4 * q + 4, :].bitcast(I32)
             )
-        nc.sync.dma_start(table_words[:, T // 4 :], x_rows[:, T // 4 :])
-        nc.sync.dma_start(wa_raw[:], wa_rows)
+        nc.sync.dma_start(table_words[:, X_FIRST :], x_rows[:, X_FIRST :])
+        nc.sync.dma_start(wa_raw[0][:], wa_rows[:, :, :HALF])
         nc.sync.dma_start(fl_sb[:], fl)
+        nc.sync.dma_start(wa_raw[1][:], wa_rows[:, :, HALF : HALF + P])
+        nc.sync.dma_start(wa_raw[2][:], wa_rows[:, :, HALF + P :])
         for h in range(2):
             nc.sync.dma_start(w1_raw[h][:], w1_rows[:, :, h * HALF : (h + 1) * HALF])
 
@@ -74,98 +88,97 @@ def tile_picked_tokmixl_relu_p_kernel(tc, x_words, x_scales, wa, gt, w1, offs, f
             in_=picked_scales[:].rearrange("p (c i t) -> p c t i", t=PACK, i=16),
         )
 
-        picked_words = [keep.tile([P, S // 2], U32, name=f"picked_words{g}", align_bytes=64) for g in range(2)]
-        for g in range(2):
-            nc.vector.tensor_copy(
-                picked_words[g][:], table_words[:].bitcast(U32).indirect(offs_sb[:, g * 16 : (g + 1) * 16])
-            )
-        for g in range(2):
-            nc.vector.tensor_copy(
-                out=x_codes[:].bitcast(I32).rearrange("p (t g m) -> p g m t", t=PACK, g=2)[:, g],
-                in_=picked_words[g][:].bitcast(I32).rearrange("p (m t) -> p m t", t=PACK),
-            )
+        nc.vector.tensor_copy(
+            x_codes[:].rearrange("p (t m) -> p m t", t=PACK), table_words[:].bitcast(U32).indirect(offs_sb[:])
+        )
 
-        gt_wide = keep.tile([P, 2, V], F32, name="gt_wide")
-        nc.scalar.copy(out=gt_wide[:], in_=gt_sb[:, 2:].unsqueeze(2).to_broadcast([P, 2, V]))
+        gt_wide = keep.tile([P, PACK, V], F32, name="gt_wide")
+        nc.scalar.copy(out=gt_wide[:], in_=gt_sb[:].unsqueeze(2).to_broadcast([P, PACK, V]))
 
         wa_codes = keep.tile([P, H], U32, name="wa_codes", align_bytes=64)
         wa_sc = keep.tile([P, H], U8, name="wa_sc", align_bytes=64)
-        wa_grouped = keep.tile([P, PACK * H], BF16, name="wa_grouped", align_bytes=64)
-        interleave(nc.scalar.copy, wa_grouped, wa_raw, 0, 128)
-        interleave(nc.vector.tensor_copy, wa_grouped, wa_raw, 128, 256)
-        interleave(nc.scalar.copy, wa_grouped, wa_raw, 256, 320)
-        interleave(nc.vector.tensor_copy, wa_grouped, wa_raw, 320, H)
-        for lo in (0, HALF):
-            quantize(nc, wa_codes, wa_sc, wa_grouped, lo, lo + HALF)
+        wa_grouped = shared.tile([P, PACK * H], BF16, name="wa_grouped", align_bytes=64, offset=4 * H * PACK)
+        interleave(nc.scalar.copy, wa_grouped, wa_raw[0], 160, HALF)
+        interleave(nc.vector.tensor_copy, wa_grouped, wa_raw[0], 0, P)
+        interleave(nc.vector.tensor_copy, wa_grouped, wa_raw[0], P, 160)
+        interleave(nc.scalar.copy, wa_grouped, wa_raw[1], 0, P, HALF)
+        quantize(nc, wa_codes, wa_sc, wa_grouped, 0, P)
+        quantize(nc, wa_codes, wa_sc, wa_grouped, P, HALF)
+        interleave(nc.vector.tensor_copy, wa_grouped, wa_raw[2], 0, P, HALF + P)
+        quantize(nc, wa_codes, wa_sc, wa_grouped, HALF, HALF + P)
+        quantize(nc, wa_codes, wa_sc, wa_grouped, HALF + P, H)
 
-        bank = {(h, t): PACK * h + t for h in range(2) for t in range(PACK)}
-        bank[0, 2] = bank[1, 0]
-        bank[0, 3] = bank[1, 1]
-        y = [keep.tile([P, H], F32, name=f"y{t}", align_bytes=64) for t in range(PACK)]
-        acc = {}
+        y = [shared.tile([P, H], F32, name=f"y{t}", align_bytes=64, offset=4 * H * t) for t in range(PACK)]
 
-        def project(h, t):
-            acc[h, t] = psum.tile([P, HALF], F32, name=f"acc{h}{t}", tag=f"bank{bank[h, t]}")
-            nc.tensor.matmul_mx(
-                out=acc[h, t][:],
-                lhsT=x_codes[:, t * P : (t + 1) * P].bitcast(FP8X4),
-                lhsT_scale=x_sc[:, t * P : (t + 1) * P],
-                rhs=wa_codes[:, h * HALF : (h + 1) * HALF].bitcast(FP8X4),
-                rhs_scale=wa_sc[:, h * HALF : (h + 1) * HALF],
-                start=True,
-                stop=True,
-            )
+        def project(t, lo, hi, bank, width=H):
+            acc = psum.tile([P, hi - lo], F32, name=f"acc{t}_{lo}", tag=f"bank{bank}")
+            for a in range(lo, hi, width):
+                b = min(a + width, hi)
+                nc.tensor.matmul_mx(
+                    out=acc[:, a - lo : b - lo],
+                    lhsT=x_codes[:, t * P : (t + 1) * P].bitcast(FP8X4),
+                    lhsT_scale=x_sc[:, t * P : (t + 1) * P],
+                    rhs=wa_codes[:, a:b].bitcast(FP8X4),
+                    rhs_scale=wa_sc[:, a:b],
+                    start=True,
+                    stop=True,
+                )
+            nc.scalar.activation(out=y[t][:, lo:hi], in_=acc[:], func=ACT.Relu)
 
-        w1_grouped = [keep.tile([P, PACK * HALF], BF16, name="w1_grouped0", align_bytes=64)]
-        w1_codes = [keep.tile([P, HALF], U32, name="w1_codes0", align_bytes=64)]
+        project(0, 0, HALF, 0, P)
+        project(1, 0, HALF, 1)
+        project(0, HALF, HALF + P, 2)
+        project(0, HALF + P, H, 3)
+        project(1, HALF, H, 4)
+        project(2, 0, H, 5)
+        project(3, 0, H, 6)
+
+        w1_grouped = [
+            shared.tile([P, PACK * HALF], BF16, name=f"w1_grouped{h}", align_bytes=64, offset=at)
+            for h, at in enumerate((4 * H * PACK, 0))
+        ]
+        w1_codes = [keep.tile([P, HALF], U32, name=f"w1_codes{h}", align_bytes=64) for h in range(2)]
         w1_sc = [keep.tile([P, HALF], U8, name=f"w1_sc{h}", align_bytes=64) for h in range(2)]
-        interleave(nc.vector.tensor_copy, w1_grouped[0], w1_raw[0], 0, HALF)
-        nc.vector.quantize_mx(out=w1_codes[0][:].bitcast(FP8X4), scales=w1_sc[0][:], in_=w1_grouped[0][:])
+        for lo in (0, P):
+            interleave(nc.vector.tensor_copy, w1_grouped[0], w1_raw[0], lo, lo + P)
+        for lo in (0, P):
+            quantize(nc, w1_codes[0], w1_sc[0], w1_grouped[0], lo, lo + P)
 
-        looked_up = keep.tile([P, 2, V], F32, name="looked_up", tag="w1_raw0", align_bytes=64)
         z = keep.tile([P, PACK, V], F32, name="z", align_bytes=64)
         for t in range(PACK):
-            for h in range(2):
-                project(h, t)
-                nc.scalar.activation(out=y[t][:, h * HALF : (h + 1) * HALF], in_=acc[h, t][:], func=ACT.Relu)
-            if t < 2:
-                nc.vector.tensor_copy(looked_up[:, t, :], y[t][:].indirect(fl_sb[:]))
-            else:
-                for lo, hi in ((0, V),) if t < PACK - 1 else ((0, P), (P, V)):
-                    nc.vector.tensor_tensor(
-                        z[:, t, lo:hi], y[t][:].indirect(fl_sb[:, lo // 16 : hi // 16]), gt_wide[:, t - 2, lo:hi], ALU.mult
-                    )
-        for t in range(2):
-            nc.scalar.activation(out=z[:, t, :], in_=looked_up[:, t, :], func=ACT.Copy, scale=gt_sb[:, t : t + 1])
-        w1_grouped.append(keep.tile([P, PACK * HALF], BF16, name="w1_grouped1", tag="w1_raw0", align_bytes=64))
-        interleave(nc.scalar.copy, w1_grouped[1], w1_raw[1], 0, HALF)
+            for lo, hi in ((0, V),) if t < PACK - 1 else ((0, P), (P, V)):
+                nc.vector.tensor_tensor(
+                    z[:, t, lo:hi], y[t][:].indirect(fl_sb[:, lo // 16 : hi // 16]), gt_wide[:, t, lo:hi], ALU.mult
+                )
+        for lo in (0, P):
+            interleave(nc.scalar.copy, w1_grouped[1], w1_raw[1], lo, lo + P)
 
-        z_grouped = keep.tile([P, PACK * V], BF16, name="z_grouped", tag="z_grouped", align_bytes=64)
         z_codes = keep.tile([P, V], U32, name="z_codes", align_bytes=64)
         z_sc = keep.tile([P, V], U8, name="z_sc", align_bytes=64)
-        for lo in (0, P):
-            interleave(nc.vector.tensor_copy, z_grouped, z, lo, lo + P)
-        for lo in (0, P):
-            quantize(nc, z_codes, z_sc, z_grouped, lo, lo + P)
-        w1_codes.append(keep.tile([P, HALF], U32, name="w1_codes1", tag="z_grouped", align_bytes=64))
-        for lo in (0, P):
+        for g, tag in enumerate(("z_grouped0", "z_grouped1")):
+            lo = g * P
+            z_grouped = keep.tile([P, PACK * P], BF16, name=f"z_grouped{g}", tag=tag, align_bytes=64)
+            interleave(nc.scalar.copy if g else nc.vector.tensor_copy, z_grouped, z, lo, lo + P, -lo)
             quantize(nc, w1_codes[1], w1_sc[1], w1_grouped[1], lo, lo + P)
+            nc.vector.quantize_mx(out=z_codes[:, lo : lo + P].bitcast(FP8X4), scales=z_sc[:, lo : lo + P], in_=z_grouped[:])
 
-        total = [psum.tile([P, V], F32, name=f"total{u}", tag=f"bank{u}") for u in range(N // P)]
-        pieces = [(u, lo, lo + P) for lo in (0, P) for u in range(2)] + [(u, 0, V) for u in range(2, N // P)]
-        for u, lo, hi in pieces:
-            cols = slice((u % 2) * P, (u % 2 + 1) * P)
-            nc.tensor.matmul_mx(
-                out=total[u][:, lo:hi],
-                lhsT=w1_codes[u // 2][:, cols].bitcast(FP8X4),
-                lhsT_scale=w1_sc[u // 2][:, cols],
-                rhs=z_codes[:, lo:hi].bitcast(FP8X4),
-                rhs_scale=z_sc[:, lo:hi],
-                start=True,
-                stop=True,
-            )
-        for u in range(N // P):
-            result = keep.tile([P, V], F32, name=f"result{u}")
-            copy = nc.vector.tensor_copy if u % 2 else nc.scalar.copy
-            copy(out=result[:], in_=total[u][:])
-            nc.sync.dma_start(out[u * P : (u + 1) * P, :], result[:])
+        out_rows = out.rearrange("(u p) v -> p u v", p=P)
+        groups = [(0, 0, 2), (0, 2, 2)] + [(P, u, 1) for u in range(4)]
+        for n, (lo, first, count) in enumerate(groups):
+            total = psum.tile([P, count, P], F32, name=f"total{n}", tag=f"bank{n}")
+            for j in range(count):
+                u = first + j
+                cols = slice((u % 2) * P, (u % 2 + 1) * P)
+                nc.tensor.matmul_mx(
+                    out=total[:, j, :],
+                    lhsT=w1_codes[u // 2][:, cols].bitcast(FP8X4),
+                    lhsT_scale=w1_sc[u // 2][:, cols],
+                    rhs=z_codes[:, lo : lo + P].bitcast(FP8X4),
+                    rhs_scale=z_sc[:, lo : lo + P],
+                    start=True,
+                    stop=True,
+                )
+            result = keep.tile([P, count, P], F32, name=f"result{n}")
+            copy = nc.vector.tensor_copy if n in (3, 5) else nc.scalar.copy
+            copy(out=result[:], in_=total[:])
+            nc.sync.dma_start(out_rows[:, first : first + count, lo : lo + P], result[:])

@@ -21,7 +21,9 @@ HALF = 256
 
 
 RUN = 4
-X_FIRST = T // 4
+PLAIN = 2
+WA_ON_SCALAR = (128, 96)
+X_FIRST = 3 * T // 8
 
 
 def interleave(copy, grouped, raw, lo, hi, at=0):
@@ -51,11 +53,10 @@ def tile_picked_tokmixl_relu_p_kernel(tc, x_words, x_scales, wa, gt, w1, offs, f
         gt_sb = keep.tile([P, PACK], F32, name="gt_sb")
         wa_raw = [
             keep.tile([P, PACK, HALF], F32, name="wa_raw0", align_bytes=64),
-            shared.tile([P, PACK, P], F32, name="wa_raw1", align_bytes=64, offset=0),
-            keep.tile([P, PACK, P], F32, name="wa_raw2", align_bytes=64),
+            shared.tile([P, PACK, HALF], F32, name="wa_raw1", align_bytes=64, offset=0),
         ]
         w1_raw = [
-            keep.tile([P, PACK, HALF], F32, name="w1_raw0", align_bytes=64),
+            keep.tile([P, PACK, HALF], F32, name="w1_raw0", tag="w1_raw0", align_bytes=64),
             keep.tile([P, PACK, HALF], F32, name="w1_raw1", tag="w1_raw1", align_bytes=64),
         ]
 
@@ -67,17 +68,16 @@ def tile_picked_tokmixl_relu_p_kernel(tc, x_words, x_scales, wa, gt, w1, offs, f
         nc.sync.dma_start(offs_sb[:], offs)
         nc.scalar.dma_start(gt_sb[:], gt.rearrange("(p t) o -> p (t o)", t=PACK))
         for q in range(4):
-            queue = nc.sync if q < 2 else nc.scalar
-            queue.dma_start(
+            nc.sync.dma_start(
                 table_scales[32 * q : 32 * q + 4, :].bitcast(I32), x_scales[0, 4 * q : 4 * q + 4, :].bitcast(I32)
             )
         nc.sync.dma_start(table_words[:, X_FIRST :], x_rows[:, X_FIRST :])
         nc.sync.dma_start(wa_raw[0][:], wa_rows[:, :, :HALF])
-        nc.sync.dma_start(fl_sb[:], fl)
-        nc.sync.dma_start(wa_raw[1][:], wa_rows[:, :, HALF : HALF + P])
-        nc.sync.dma_start(wa_raw[2][:], wa_rows[:, :, HALF + P :])
+        nc.sync.dma_start(wa_raw[1][:], wa_rows[:, :, HALF:])
         for h in range(2):
             nc.sync.dma_start(w1_raw[h][:], w1_rows[:, :, h * HALF : (h + 1) * HALF])
+            if h == 0:
+                nc.sync.dma_start(fl_sb[:], fl)
 
         picked_scales = keep.tile([P, S], U8, name="picked_scales", align_bytes=64)
         x_sc = keep.tile([P, S], U8, name="x_sc", align_bytes=64)
@@ -92,21 +92,20 @@ def tile_picked_tokmixl_relu_p_kernel(tc, x_words, x_scales, wa, gt, w1, offs, f
             x_codes[:].rearrange("p (t m) -> p m t", t=PACK), table_words[:].bitcast(U32).indirect(offs_sb[:])
         )
 
-        gt_wide = keep.tile([P, PACK, V], F32, name="gt_wide")
-        nc.scalar.copy(out=gt_wide[:], in_=gt_sb[:].unsqueeze(2).to_broadcast([P, PACK, V]))
+        gt_wide = keep.tile([P, PACK - PLAIN, V], F32, name="gt_wide")
+        nc.scalar.copy(out=gt_wide[:], in_=gt_sb[:, PLAIN:].unsqueeze(2).to_broadcast([P, PACK - PLAIN, V]))
 
         wa_codes = keep.tile([P, H], U32, name="wa_codes", align_bytes=64)
         wa_sc = keep.tile([P, H], U8, name="wa_sc", align_bytes=64)
         wa_grouped = shared.tile([P, PACK * H], BF16, name="wa_grouped", align_bytes=64, offset=4 * H * PACK)
-        interleave(nc.scalar.copy, wa_grouped, wa_raw[0], 160, HALF)
-        interleave(nc.vector.tensor_copy, wa_grouped, wa_raw[0], 0, P)
-        interleave(nc.vector.tensor_copy, wa_grouped, wa_raw[0], P, 160)
-        interleave(nc.scalar.copy, wa_grouped, wa_raw[1], 0, P, HALF)
-        quantize(nc, wa_codes, wa_sc, wa_grouped, 0, P)
-        quantize(nc, wa_codes, wa_sc, wa_grouped, P, HALF)
-        interleave(nc.vector.tensor_copy, wa_grouped, wa_raw[2], 0, P, HALF + P)
-        quantize(nc, wa_codes, wa_sc, wa_grouped, HALF, HALF + P)
-        quantize(nc, wa_codes, wa_sc, wa_grouped, HALF + P, H)
+        for h in range(2):
+            split = HALF - WA_ON_SCALAR[h]
+            interleave(nc.scalar.copy, wa_grouped, wa_raw[h], split, HALF, h * HALF)
+            interleave(nc.vector.tensor_copy, wa_grouped, wa_raw[h], 0, P, h * HALF)
+            if split > P:
+                interleave(nc.vector.tensor_copy, wa_grouped, wa_raw[h], P, split, h * HALF)
+            for lo in (h * HALF, h * HALF + P):
+                quantize(nc, wa_codes, wa_sc, wa_grouped, lo, lo + P)
 
         y = [shared.tile([P, H], F32, name=f"y{t}", align_bytes=64, offset=4 * H * t) for t in range(PACK)]
 
@@ -125,7 +124,7 @@ def tile_picked_tokmixl_relu_p_kernel(tc, x_words, x_scales, wa, gt, w1, offs, f
                 )
             nc.scalar.activation(out=y[t][:, lo:hi], in_=acc[:], func=ACT.Relu)
 
-        project(0, 0, HALF, 0, P)
+        project(0, 0, HALF, 0)
         project(1, 0, HALF, 1)
         project(0, HALF, HALF + P, 2)
         project(0, HALF + P, H, 3)
@@ -135,7 +134,7 @@ def tile_picked_tokmixl_relu_p_kernel(tc, x_words, x_scales, wa, gt, w1, offs, f
 
         w1_grouped = [
             shared.tile([P, PACK * HALF], BF16, name=f"w1_grouped{h}", align_bytes=64, offset=at)
-            for h, at in enumerate((4 * H * PACK, 0))
+            for h, at in enumerate((4 * H * PACK, 4 * H))
         ]
         w1_codes = [keep.tile([P, HALF], U32, name=f"w1_codes{h}", align_bytes=64) for h in range(2)]
         w1_sc = [keep.tile([P, HALF], U8, name=f"w1_sc{h}", align_bytes=64) for h in range(2)]
@@ -144,41 +143,50 @@ def tile_picked_tokmixl_relu_p_kernel(tc, x_words, x_scales, wa, gt, w1, offs, f
         for lo in (0, P):
             quantize(nc, w1_codes[0], w1_sc[0], w1_grouped[0], lo, lo + P)
 
-        z = keep.tile([P, PACK, V], F32, name="z", align_bytes=64)
-        for t in range(PACK):
+        z = keep.tile([P, PACK, V], F32, name="z", tag="w1_raw0", align_bytes=64)
+        for t in range(PLAIN):
+            nc.vector.tensor_copy(z[:, t, :], y[t][:].indirect(fl_sb[:]))
+        for t in range(PLAIN, PACK):
             for lo, hi in ((0, V),) if t < PACK - 1 else ((0, P), (P, V)):
                 nc.vector.tensor_tensor(
-                    z[:, t, lo:hi], y[t][:].indirect(fl_sb[:, lo // 16 : hi // 16]), gt_wide[:, t, lo:hi], ALU.mult
+                    z[:, t, lo:hi], y[t][:].indirect(fl_sb[:, lo // 16 : hi // 16]), gt_wide[:, t - PLAIN, lo:hi], ALU.mult
                 )
+        for t in range(PLAIN):
+            nc.scalar.activation(out=z[:, t, :], in_=z[:, t, :], func=ACT.Copy, scale=gt_sb[:, t : t + 1])
         for lo in (0, P):
             interleave(nc.scalar.copy, w1_grouped[1], w1_raw[1], lo, lo + P)
 
         z_codes = keep.tile([P, V], U32, name="z_codes", align_bytes=64)
         z_sc = keep.tile([P, V], U8, name="z_sc", align_bytes=64)
-        for g, tag in enumerate(("z_grouped0", "z_grouped1")):
-            lo = g * P
-            z_grouped = keep.tile([P, PACK * P], BF16, name=f"z_grouped{g}", tag=tag, align_bytes=64)
-            interleave(nc.scalar.copy if g else nc.vector.tensor_copy, z_grouped, z, lo, lo + P, -lo)
+        z_grouped = keep.tile([P, PACK * V], BF16, name="z_grouped", tag="z_grouped", align_bytes=64)
+        for lo in (0, P):
+            interleave(nc.vector.tensor_copy, z_grouped, z, lo, lo + P)
+        for lo in (0, P):
+            quantize(nc, z_codes, z_sc, z_grouped, lo, lo + P)
+        for lo in (0, P):
             quantize(nc, w1_codes[1], w1_sc[1], w1_grouped[1], lo, lo + P)
-            nc.vector.quantize_mx(out=z_codes[:, lo : lo + P].bitcast(FP8X4), scales=z_sc[:, lo : lo + P], in_=z_grouped[:])
 
-        out_rows = out.rearrange("(u p) v -> p u v", p=P)
-        groups = [(0, 0, 2), (0, 2, 2)] + [(P, u, 1) for u in range(4)]
-        for n, (lo, first, count) in enumerate(groups):
-            total = psum.tile([P, count, P], F32, name=f"total{n}", tag=f"bank{n}")
-            for j in range(count):
-                u = first + j
-                cols = slice((u % 2) * P, (u % 2 + 1) * P)
-                nc.tensor.matmul_mx(
-                    out=total[:, j, :],
-                    lhsT=w1_codes[u // 2][:, cols].bitcast(FP8X4),
-                    lhsT_scale=w1_sc[u // 2][:, cols],
-                    rhs=z_codes[:, lo : lo + P].bitcast(FP8X4),
-                    rhs_scale=z_sc[:, lo : lo + P],
-                    start=True,
-                    stop=True,
-                )
-            result = keep.tile([P, count, P], F32, name=f"result{n}")
-            copy = nc.vector.tensor_copy if n in (3, 5) else nc.scalar.copy
-            copy(out=result[:], in_=total[:])
-            nc.sync.dma_start(out_rows[:, first : first + count, lo : lo + P], result[:])
+        total = [psum.tile([P, V], F32, name=f"total{u}", tag=f"bank{u}") for u in range(3)]
+        last = [psum.tile([P, P], F32, name=f"last{g}", tag=f"bank{3 + g}") for g in range(2)]
+        pieces = [(u, lo, lo + P, total[u][:, lo : lo + P]) for lo in (0, P) for u in range(2)]
+        pieces += [(2, 0, V, total[2][:])] + [(3, g * P, (g + 1) * P, last[g][:]) for g in range(2)]
+        for u, lo, hi, acc in pieces:
+            cols = slice((u % 2) * P, (u % 2 + 1) * P)
+            nc.tensor.matmul_mx(
+                out=acc,
+                lhsT=w1_codes[u // 2][:, cols].bitcast(FP8X4),
+                lhsT_scale=w1_sc[u // 2][:, cols],
+                rhs=z_codes[:, lo:hi].bitcast(FP8X4),
+                rhs_scale=z_sc[:, lo:hi],
+                start=True,
+                stop=True,
+            )
+        for u in range(N // P):
+            result = keep.tile([P, V], F32, name=f"result{u}")
+            if u < 3:
+                copy = nc.vector.tensor_copy if u % 2 else nc.scalar.copy
+                copy(out=result[:], in_=total[u][:])
+            else:
+                nc.vector.tensor_copy(out=result[:, :P], in_=last[0][:])
+                nc.vector.tensor_copy(out=result[:, P:], in_=last[1][:])
+            nc.sync.dma_start(out[u * P : (u + 1) * P, :], result[:])

@@ -22,8 +22,6 @@ HALF = 256
 
 RUN = 4
 PLAIN = 2
-WA_ON_SCALAR = (128, 96)
-X_FIRST = 3 * T // 8
 
 
 def interleave(copy, grouped, raw, lo, hi, at=0):
@@ -48,8 +46,8 @@ def tile_picked_tokmixl_relu_p_kernel(tc, x_words, x_scales, wa, gt, w1, offs, f
 
         offs_sb = keep.tile([P, S // 16], U16, name="offs_sb")
         fl_sb = keep.tile([P, V // 16], U16, name="fl_sb")
-        table_words = keep.tile([P, T], I32, name="table_words", align_bytes=64)
-        table_scales = keep.tile([P, T], U8, name="table_scales", align_bytes=64)
+        table_words = keep.tile([P, T], I32, name="table_words", tag="table_words", align_bytes=64)
+        table_scales = keep.tile([P, T], U8, name="table_scales", tag="table_scales", align_bytes=64)
         gt_sb = keep.tile([P, PACK], F32, name="gt_sb")
         wa_raw = [
             keep.tile([P, PACK, HALF], F32, name="wa_raw0", align_bytes=64),
@@ -64,15 +62,14 @@ def tile_picked_tokmixl_relu_p_kernel(tc, x_words, x_scales, wa, gt, w1, offs, f
         wa_rows = wa.rearrange("(p t) c -> p t c", t=PACK)
         w1_rows = w1.rearrange("(p t) c -> p t c", t=PACK)
         nc.vector.memset(table_scales[:].bitcast(I32), 0)
-        nc.sync.dma_start(table_words[:, : X_FIRST], x_rows[:, : X_FIRST])
+        nc.sync.dma_start(wa_raw[0][:], wa_rows[:, :, :HALF])
         nc.sync.dma_start(offs_sb[:], offs)
         nc.scalar.dma_start(gt_sb[:], gt.rearrange("(p t) o -> p (t o)", t=PACK))
         for q in range(4):
             nc.sync.dma_start(
                 table_scales[32 * q : 32 * q + 4, :].bitcast(I32), x_scales[0, 4 * q : 4 * q + 4, :].bitcast(I32)
             )
-        nc.sync.dma_start(table_words[:, X_FIRST :], x_rows[:, X_FIRST :])
-        nc.sync.dma_start(wa_raw[0][:], wa_rows[:, :, :HALF])
+        nc.sync.dma_start(table_words[:], x_rows)
         nc.sync.dma_start(wa_raw[1][:], wa_rows[:, :, HALF:])
         for h in range(2):
             nc.sync.dma_start(w1_raw[h][:], w1_rows[:, :, h * HALF : (h + 1) * HALF])
@@ -95,17 +92,18 @@ def tile_picked_tokmixl_relu_p_kernel(tc, x_words, x_scales, wa, gt, w1, offs, f
         gt_wide = keep.tile([P, PACK - PLAIN, V], F32, name="gt_wide")
         nc.scalar.copy(out=gt_wide[:], in_=gt_sb[:, PLAIN:].unsqueeze(2).to_broadcast([P, PACK - PLAIN, V]))
 
-        wa_codes = keep.tile([P, H], U32, name="wa_codes", align_bytes=64)
+        wa_codes = keep.tile([P, H], U32, name="wa_codes", tag="table_scales", align_bytes=64)
         wa_sc = keep.tile([P, H], U8, name="wa_sc", align_bytes=64)
         wa_grouped = shared.tile([P, PACK * H], BF16, name="wa_grouped", align_bytes=64, offset=4 * H * PACK)
-        for h in range(2):
-            split = HALF - WA_ON_SCALAR[h]
-            interleave(nc.scalar.copy, wa_grouped, wa_raw[h], split, HALF, h * HALF)
-            interleave(nc.vector.tensor_copy, wa_grouped, wa_raw[h], 0, P, h * HALF)
-            if split > P:
-                interleave(nc.vector.tensor_copy, wa_grouped, wa_raw[h], P, split, h * HALF)
-            for lo in (h * HALF, h * HALF + P):
-                quantize(nc, wa_codes, wa_sc, wa_grouped, lo, lo + P)
+        wa_third = keep.tile([P, PACK * P], BF16, name="wa_third", tag="table_words", align_bytes=64)
+        interleave(nc.scalar.copy, wa_grouped, wa_raw[0], 0, HALF)
+        quantize(nc, wa_codes, wa_sc, wa_grouped, 0, HALF)
+        interleave(nc.scalar.copy, wa_grouped, wa_raw[1], P, HALF, HALF)
+        interleave(nc.vector.tensor_copy, wa_third, wa_raw[1], 0, P)
+        nc.vector.quantize_mx(
+            out=wa_codes[:, HALF : HALF + P].bitcast(FP8X4), scales=wa_sc[:, HALF : HALF + P], in_=wa_third[:]
+        )
+        quantize(nc, wa_codes, wa_sc, wa_grouped, HALF + P, H)
 
         y = [shared.tile([P, H], F32, name=f"y{t}", align_bytes=64, offset=4 * H * t) for t in range(PACK)]
 

@@ -64,12 +64,10 @@ def tile_picked_tokmixl_relu_p_kernel(tc, x_words, x_scales, wa, gt, w1, offs, f
         nc.vector.memset(table_scales[:].bitcast(I32), 0)
         nc.sync.dma_start(wa_raw[0][:], wa_rows[:, :, :HALF])
         nc.sync.dma_start(offs_sb[:], offs)
-        nc.scalar.dma_start(gt_sb[:], gt.rearrange("(p t) o -> p (t o)", t=PACK))
-        for q in range(4):
-            nc.sync.dma_start(
-                table_scales[32 * q : 32 * q + 4, :].bitcast(I32), x_scales[0, 4 * q : 4 * q + 4, :].bitcast(I32)
-            )
+        for r in range(4):
+            nc.sync.dma_start(table_scales[r:P:32, :].bitcast(I32), x_scales[0, r:16:4, :].bitcast(I32))
         nc.sync.dma_start(table_words[:], x_rows)
+        nc.sync.dma_start(gt_sb[:], gt.rearrange("(p t) o -> p (t o)", t=PACK))
         nc.sync.dma_start(wa_raw[1][:], wa_rows[:, :, HALF:])
         for h in range(2):
             nc.sync.dma_start(w1_raw[h][:], w1_rows[:, :, h * HALF : (h + 1) * HALF])

@@ -128,6 +128,18 @@ def tile_picked_tokmixl_relu_p_kernel(tc, x_words, x_scales, wa, gt, w1, offs, f
         project(2, 0, H, 5)
         project(3, 0, H, 6)
 
+        for g in range(2):
+            unread = psum.tile([64, H], F32, name=f"unread{g}", tag="bank6")
+            nc.tensor.matmul_mx(
+                out=unread[:],
+                lhsT=x_codes[:, g * 64 : (g + 1) * 64].bitcast(FP8X4),
+                lhsT_scale=x_sc[:, g * 64 : (g + 1) * 64],
+                rhs=wa_codes[:].bitcast(FP8X4),
+                rhs_scale=wa_sc[:],
+                start=True,
+                stop=True,
+            )
+
         w1_grouped = [
             shared.tile([P, PACK * HALF], BF16, name=f"w1_grouped{h}", align_bytes=64, offset=at)
             for h, at in enumerate((4 * H * PACK, 4 * H))
@@ -162,14 +174,13 @@ def tile_picked_tokmixl_relu_p_kernel(tc, x_words, x_scales, wa, gt, w1, offs, f
         for lo in (0, P):
             quantize(nc, w1_codes[1], w1_sc[1], w1_grouped[1], lo, lo + P)
 
-        total = [psum.tile([P, V], F32, name=f"total{u}", tag=f"bank{u}") for u in range(3)]
-        last = [psum.tile([P, P], F32, name=f"last{g}", tag=f"bank{3 + g}") for g in range(2)]
-        pieces = [(u, lo, lo + P, total[u][:, lo : lo + P]) for lo in (0, P) for u in range(2)]
-        pieces += [(2, 0, V, total[2][:])] + [(3, g * P, (g + 1) * P, last[g][:]) for g in range(2)]
-        for u, lo, hi, acc in pieces:
+        banks = ((0, 0, P, 0), (1, 0, P, 2), (0, P, V, 1), (1, P, V, 3), (2, 0, V, 4), (3, 0, P, 5), (3, P, V, 7))
+        acc = {}
+        for u, lo, hi, bank in banks:
             cols = slice((u % 2) * P, (u % 2 + 1) * P)
+            acc[u, lo] = psum.tile([P, hi - lo], F32, name=f"total{u}_{lo}", tag=f"bank{bank}")
             nc.tensor.matmul_mx(
-                out=acc,
+                out=acc[u, lo][:],
                 lhsT=w1_codes[u // 2][:, cols].bitcast(FP8X4),
                 lhsT_scale=w1_sc[u // 2][:, cols],
                 rhs=z_codes[:, lo:hi].bitcast(FP8X4),
@@ -177,12 +188,16 @@ def tile_picked_tokmixl_relu_p_kernel(tc, x_words, x_scales, wa, gt, w1, offs, f
                 start=True,
                 stop=True,
             )
-        for u in range(N // P):
-            result = keep.tile([P, V], F32, name=f"result{u}")
-            if u < 3:
-                copy = nc.vector.tensor_copy if u % 2 else nc.scalar.copy
-                copy(out=result[:], in_=total[u][:])
-            else:
-                nc.vector.tensor_copy(out=result[:, :P], in_=last[0][:])
-                nc.vector.tensor_copy(out=result[:, P:], in_=last[1][:])
-            nc.sync.dma_start(out[u * P : (u + 1) * P, :], result[:])
+        result = [keep.tile([P, V], F32, name=f"result{u}") for u in range(N // P)]
+        for u, lo, hi, copy in (
+            (0, 0, P, nc.scalar.copy),
+            (0, P, V, nc.scalar.copy),
+            (1, 0, P, nc.scalar.copy),
+            (1, P, V, nc.vector.tensor_copy),
+            (2, 0, V, nc.vector.tensor_copy),
+            (3, 0, P, nc.scalar.copy),
+            (3, P, V, nc.vector.tensor_copy),
+        ):
+            copy(out=result[u][:, lo:hi], in_=acc[u, lo][:])
+            if hi == V:
+                nc.sync.dma_start(out[u * P : (u + 1) * P, :], result[u][:])

@@ -105,9 +105,9 @@ def tile_picked_tokmixl_relu_p_kernel(tc, x_words, x_scales, wa, gt, w1, offs, f
 
         y = [shared.tile([P, H], F32, name=f"y{t}", align_bytes=64, offset=4 * H * t) for t in range(PACK)]
 
-        def project(t, lo, hi, bank, width=H):
+        def project(t, lo, hi, bank, width=P):
             acc = psum.tile([P, hi - lo], F32, name=f"acc{t}_{lo}", tag=f"bank{bank}")
-            for a in range(lo, hi, width):
+            for a in reversed(range(lo, hi, width)):
                 b = min(a + width, hi)
                 nc.tensor.matmul_mx(
                     out=acc[:, a - lo : b - lo],
@@ -179,25 +179,25 @@ def tile_picked_tokmixl_relu_p_kernel(tc, x_words, x_scales, wa, gt, w1, offs, f
         for u, lo, hi, bank in banks:
             cols = slice((u % 2) * P, (u % 2 + 1) * P)
             acc[u, lo] = psum.tile([P, hi - lo], F32, name=f"total{u}_{lo}", tag=f"bank{bank}")
-            nc.tensor.matmul_mx(
-                out=acc[u, lo][:],
-                lhsT=w1_codes[u // 2][:, cols].bitcast(FP8X4),
-                lhsT_scale=w1_sc[u // 2][:, cols],
-                rhs=z_codes[:, lo:hi].bitcast(FP8X4),
-                rhs_scale=z_sc[:, lo:hi],
-                start=True,
-                stop=True,
-            )
-        result = [keep.tile([P, V], F32, name=f"result{u}") for u in range(N // P)]
-        for u, lo, hi, copy in (
-            (0, 0, P, nc.scalar.copy),
-            (0, P, V, nc.scalar.copy),
-            (1, 0, P, nc.scalar.copy),
-            (1, P, V, nc.vector.tensor_copy),
-            (2, 0, V, nc.vector.tensor_copy),
-            (3, 0, P, nc.scalar.copy),
-            (3, P, V, nc.vector.tensor_copy),
-        ):
-            copy(out=result[u][:, lo:hi], in_=acc[u, lo][:])
-            if hi == V:
-                nc.sync.dma_start(out[u * P : (u + 1) * P, :], result[u][:])
+            for a in range(lo, hi, P):
+                nc.tensor.matmul_mx(
+                    out=acc[u, lo][:, a - lo : a - lo + P],
+                    lhsT=w1_codes[u // 2][:, cols].bitcast(FP8X4),
+                    lhsT_scale=w1_sc[u // 2][:, cols],
+                    rhs=z_codes[:, a : a + P].bitcast(FP8X4),
+                    rhs_scale=z_sc[:, a : a + P],
+                    start=True,
+                    stop=True,
+                )
+        first_rows = out[: 2 * P, :].rearrange("(u p) v -> p u v", p=P)
+        for lo, copies in ((0, (nc.scalar.copy, nc.scalar.copy)), (P, (nc.scalar.copy, nc.vector.tensor_copy))):
+            pair = keep.tile([P, 2, P], F32, name=f"pair{lo}")
+            for u in range(2):
+                copies[u](out=pair[:, u, :], in_=acc[u, lo][:])
+            nc.sync.dma_start(first_rows[:, :, lo : lo + P], pair[:])
+        result = [keep.tile([P, V], F32, name=f"result{u}") for u in range(2)]
+        nc.vector.tensor_copy(out=result[0][:], in_=acc[2, 0][:])
+        nc.sync.dma_start(out[2 * P : 3 * P, :], result[0][:])
+        nc.scalar.copy(out=result[1][:, :P], in_=acc[3, 0][:])
+        nc.vector.tensor_copy(out=result[1][:, P:], in_=acc[3, P][:])
+        nc.sync.dma_start(out[3 * P :, :], result[1][:])

@@ -74,15 +74,9 @@ def tile_picked_tokmixl_relu_p_kernel(tc, x_words, x_scales, wa, gt, w1, offs, f
             if h == 0:
                 nc.sync.dma_start(fl_sb[:], fl)
 
-        picked_scales = keep.tile([P, S], U8, name="picked_scales", align_bytes=64)
         x_sc = keep.tile([P, S], U8, name="x_sc", align_bytes=64)
         x_codes = keep.tile([P, S], U32, name="x_codes", align_bytes=64)
-        nc.vector.tensor_copy(picked_scales[:], table_scales[:].indirect(offs_sb[:]))
-        nc.vector.tensor_copy(
-            out=x_sc[:].rearrange("p (t c i) -> p c t i", t=PACK, i=16),
-            in_=picked_scales[:].rearrange("p (c i t) -> p c t i", t=PACK, i=16),
-        )
-
+        nc.vector.tensor_copy(x_sc[:].rearrange("p (t m) -> p m t", t=PACK), table_scales[:].indirect(offs_sb[:]))
         nc.vector.tensor_copy(
             x_codes[:].rearrange("p (t m) -> p m t", t=PACK), table_words[:].bitcast(U32).indirect(offs_sb[:])
         )
@@ -120,20 +114,20 @@ def tile_picked_tokmixl_relu_p_kernel(tc, x_words, x_scales, wa, gt, w1, offs, f
                 )
             nc.scalar.activation(out=y[t][:, lo:hi], in_=acc[:], func=ACT.Relu)
 
-        project(0, 0, HALF, 0)
-        project(1, 0, HALF, 1)
+        project(0, 0, HALF, 0, HALF)
+        project(1, 0, HALF, 1, HALF)
         project(0, HALF, HALF + P, 2)
         project(0, HALF + P, H, 3)
-        project(1, HALF, H, 4)
-        project(2, 0, H, 5)
-        project(3, 0, H, 6)
+        project(1, HALF, H, 4, HALF)
+        project(2, 0, H, 5, H)
+        project(3, 0, H, 6, H)
 
         for g in range(2):
-            unread = psum.tile([64, H], F32, name=f"unread{g}", tag="bank6")
+            unread = psum.tile([32, H], F32, name=f"unread{g}", tag="bank6")
             nc.tensor.matmul_mx(
                 out=unread[:],
-                lhsT=x_codes[:, g * 64 : (g + 1) * 64].bitcast(FP8X4),
-                lhsT_scale=x_sc[:, g * 64 : (g + 1) * 64],
+                lhsT=wa_codes[:, g * 64 : g * 64 + 32].bitcast(FP8X4),
+                lhsT_scale=wa_sc[:, g * 64 : g * 64 + 32],
                 rhs=wa_codes[:].bitcast(FP8X4),
                 rhs_scale=wa_sc[:],
                 start=True,

@@ -42,6 +42,7 @@ def tile_picked_tokmixl_relu_p_kernel(tc, x_words, x_scales, wa, gt, w1, offs, f
     with ExitStack() as ctx:
         keep = ctx.enter_context(tc.tile_pool(name="keep", bufs=1))
         shared = ctx.enter_context(tc.tile_pool(name="shared", bufs=1))
+        late = ctx.enter_context(tc.tile_pool(name="late", bufs=1))
         psum = ctx.enter_context(tc.psum_pool(name="psum", bufs=1))
 
         offs_sb = keep.tile([P, S // 16], U16, name="offs_sb")
@@ -53,43 +54,44 @@ def tile_picked_tokmixl_relu_p_kernel(tc, x_words, x_scales, wa, gt, w1, offs, f
             keep.tile([P, PACK, HALF], F32, name="wa_raw0", align_bytes=64),
             shared.tile([P, PACK, HALF], F32, name="wa_raw1", align_bytes=64, offset=0),
         ]
-        w1_raw = [
-            keep.tile([P, PACK, HALF], F32, name="w1_raw0", tag="w1_raw0", align_bytes=64),
-            keep.tile([P, PACK, HALF], F32, name="w1_raw1", tag="w1_raw1", align_bytes=64),
-        ]
+        w1_raw = [late.tile([P, PACK, HALF], F32, name=f"w1_raw{h}", align_bytes=64, offset=4096 * h) for h in range(2)]
 
         x_rows = x_words[0].rearrange("p n t -> p (n t)").bitcast(I32)
         wa_rows = wa.rearrange("(p t) c -> p t c", t=PACK)
         w1_rows = w1.rearrange("(p t) c -> p t c", t=PACK)
+        nc.gpsimd.dma_start(gt_sb[:], gt.rearrange("(p t) o -> p (t o)", t=PACK))
         nc.vector.memset(table_scales[:].bitcast(I32), 0)
         nc.sync.dma_start(wa_raw[0][:], wa_rows[:, :, :HALF])
         nc.sync.dma_start(offs_sb[:], offs)
-        for r in range(4):
-            nc.sync.dma_start(table_scales[r:P:32, :].bitcast(I32), x_scales[0, r:16:4, :].bitcast(I32))
+        nc.sync.dma_start(table_scales[0:P:8, :].bitcast(I32), x_scales[0].bitcast(I32))
         nc.sync.dma_start(table_words[:], x_rows)
-        nc.sync.dma_start(gt_sb[:], gt.rearrange("(p t) o -> p (t o)", t=PACK))
         nc.sync.dma_start(wa_raw[1][:], wa_rows[:, :, HALF:])
-        for h in range(2):
-            nc.sync.dma_start(w1_raw[h][:], w1_rows[:, :, h * HALF : (h + 1) * HALF])
-            if h == 0:
-                nc.sync.dma_start(fl_sb[:], fl)
+        nc.sync.dma_start(fl_sb[:], fl)
 
+        gt_wide = keep.tile([P, PACK - PLAIN, V], F32, name="gt_wide")
+        nc.gpsimd.tensor_copy(out=gt_wide[:], in_=gt_sb[:, PLAIN:].unsqueeze(2).to_broadcast([P, PACK - PLAIN, V]))
+
+        wa_sc = keep.tile([P, H], U8, name="wa_sc", align_bytes=64)
+        wa_lead = late.tile([P, PACK * P], BF16, name="wa_lead", align_bytes=64, offset=3584)
+        wa_grouped = shared.tile([P, PACK * H], BF16, name="wa_grouped", align_bytes=64, offset=4 * H * PACK)
+        wa_third = keep.tile([P, PACK * P], BF16, name="wa_third", tag="table_words", align_bytes=64)
+        interleave(nc.scalar.copy, wa_lead, wa_raw[0], 0, P)
+        interleave(nc.scalar.copy, wa_grouped, wa_raw[0], P, HALF)
+
+        picked_sc = keep.tile([P, S], U8, name="picked_sc", align_bytes=64)
         x_sc = keep.tile([P, S], U8, name="x_sc", align_bytes=64)
         x_codes = keep.tile([P, S], U32, name="x_codes", align_bytes=64)
-        nc.vector.tensor_copy(x_sc[:].rearrange("p (t m) -> p m t", t=PACK), table_scales[:].indirect(offs_sb[:]))
+        nc.vector.tensor_copy(picked_sc[:].rearrange("p (t m) -> p m t", t=PACK), table_scales[:].indirect(offs_sb[:]))
+        for r, queue in enumerate((nc.sync, nc.scalar, nc.sync, nc.scalar)):
+            queue.dma_start(x_sc[r:P:32, :].bitcast(I32), picked_sc[8 * r : P : 32, :].bitcast(I32))
+        wa_codes = keep.tile([P, H], U32, name="wa_codes", tag="table_scales", align_bytes=64)
+        quantize(nc, wa_codes, wa_sc, wa_lead, 0, P)
+        quantize(nc, wa_codes, wa_sc, wa_grouped, P, HALF)
+        for h in range(2):
+            nc.sync.dma_start(w1_raw[h][:], w1_rows[:, :, h * HALF : (h + 1) * HALF])
         nc.vector.tensor_copy(
             x_codes[:].rearrange("p (t m) -> p m t", t=PACK), table_words[:].bitcast(U32).indirect(offs_sb[:])
         )
-
-        gt_wide = keep.tile([P, PACK - PLAIN, V], F32, name="gt_wide")
-        nc.scalar.copy(out=gt_wide[:], in_=gt_sb[:, PLAIN:].unsqueeze(2).to_broadcast([P, PACK - PLAIN, V]))
-
-        wa_codes = keep.tile([P, H], U32, name="wa_codes", tag="table_scales", align_bytes=64)
-        wa_sc = keep.tile([P, H], U8, name="wa_sc", align_bytes=64)
-        wa_grouped = shared.tile([P, PACK * H], BF16, name="wa_grouped", align_bytes=64, offset=4 * H * PACK)
-        wa_third = keep.tile([P, PACK * P], BF16, name="wa_third", tag="table_words", align_bytes=64)
-        interleave(nc.scalar.copy, wa_grouped, wa_raw[0], 0, HALF)
-        quantize(nc, wa_codes, wa_sc, wa_grouped, 0, HALF)
         interleave(nc.scalar.copy, wa_grouped, wa_raw[1], P, HALF, HALF)
         interleave(nc.vector.tensor_copy, wa_third, wa_raw[1], 0, P)
         nc.vector.quantize_mx(
@@ -145,7 +147,7 @@ def tile_picked_tokmixl_relu_p_kernel(tc, x_words, x_scales, wa, gt, w1, offs, f
         for lo in (0, P):
             quantize(nc, w1_codes[0], w1_sc[0], w1_grouped[0], lo, lo + P)
 
-        z = keep.tile([P, PACK, V], F32, name="z", tag="w1_raw0", align_bytes=64)
+        z = late.tile([P, PACK, V], F32, name="z", align_bytes=64, offset=0)
         for t in range(PLAIN):
             nc.vector.tensor_copy(z[:, t, :], y[t][:].indirect(fl_sb[:]))
         for t in range(PLAIN, PACK):

@@ -51,7 +51,7 @@ def tile_picked_tokmixl_relu_p_kernel(tc, x_words, x_scales, wa, gt, w1, offs, f
         table_scales = keep.tile([P, T], U8, name="table_scales", tag="table_scales", align_bytes=64)
         gt_sb = keep.tile([P, PACK], F32, name="gt_sb")
         wa_raw = [
-            keep.tile([P, PACK, HALF], F32, name="wa_raw0", align_bytes=64),
+            keep.tile([P, PACK, HALF], F32, name="wa_raw0", tag="wa_raw0", align_bytes=64),
             shared.tile([P, PACK, HALF], F32, name="wa_raw1", align_bytes=64, offset=0),
         ]
         w1_raw = [late.tile([P, PACK, HALF], F32, name=f"w1_raw{h}", align_bytes=64, offset=4096 * h) for h in range(2)]
@@ -68,9 +68,6 @@ def tile_picked_tokmixl_relu_p_kernel(tc, x_words, x_scales, wa, gt, w1, offs, f
         nc.sync.dma_start(wa_raw[1][:], wa_rows[:, :, HALF:])
         nc.sync.dma_start(fl_sb[:], fl)
 
-        gt_wide = keep.tile([P, PACK - PLAIN, V], F32, name="gt_wide")
-        nc.gpsimd.tensor_copy(out=gt_wide[:], in_=gt_sb[:, PLAIN:].unsqueeze(2).to_broadcast([P, PACK - PLAIN, V]))
-
         wa_sc = keep.tile([P, H], U8, name="wa_sc", align_bytes=64)
         wa_lead = late.tile([P, PACK * P], BF16, name="wa_lead", align_bytes=64, offset=3584)
         wa_grouped = shared.tile([P, PACK * H], BF16, name="wa_grouped", align_bytes=64, offset=4 * H * PACK)
@@ -84,6 +81,9 @@ def tile_picked_tokmixl_relu_p_kernel(tc, x_words, x_scales, wa, gt, w1, offs, f
         nc.vector.tensor_copy(picked_sc[:].rearrange("p (t m) -> p m t", t=PACK), table_scales[:].indirect(offs_sb[:]))
         for r, queue in enumerate((nc.sync, nc.scalar, nc.sync, nc.scalar)):
             queue.dma_start(x_sc[r:P:32, :].bitcast(I32), picked_sc[8 * r : P : 32, :].bitcast(I32))
+        gt_wide = keep.tile([P, PACK - PLAIN, V], F32, name="gt_wide", tag="wa_raw0", align_bytes=64)
+        nc.scalar.copy(out=gt_wide[:], in_=gt_sb[:, PLAIN:].unsqueeze(2).to_broadcast([P, PACK - PLAIN, V]))
+
         wa_codes = keep.tile([P, H], U32, name="wa_codes", tag="table_scales", align_bytes=64)
         quantize(nc, wa_codes, wa_sc, wa_lead, 0, P)
         quantize(nc, wa_codes, wa_sc, wa_grouped, P, HALF)

@@ -170,7 +170,7 @@ def tile_picked_tokmixl_relu_p_kernel(tc, x_words, x_scales, wa, gt, w1, offs, f
         for lo in (0, P):
             quantize(nc, w1_codes[1], w1_sc[1], w1_grouped[1], lo, lo + P)
 
-        banks = ((0, 0, P, 0), (1, 0, P, 2), (0, P, V, 1), (1, P, V, 3), (2, 0, V, 4), (3, 0, P, 5), (3, P, V, 7))
+        banks = ((0, 0, P, 0), (1, 0, P, 2), (0, P, V, 1), (1, P, V, 3), (2, 0, P, 4), (2, P, V, 6), (3, 0, P, 5), (3, P, V, 7))
         acc = {}
         for u, lo, hi, bank in banks:
             cols = slice((u % 2) * P, (u % 2 + 1) * P)
@@ -186,14 +186,17 @@ def tile_picked_tokmixl_relu_p_kernel(tc, x_words, x_scales, wa, gt, w1, offs, f
                     stop=True,
                 )
         first_rows = out[: 2 * P, :].rearrange("(u p) v -> p u v", p=P)
-        for lo, copies in ((0, (nc.scalar.copy, nc.scalar.copy)), (P, (nc.scalar.copy, nc.vector.tensor_copy))):
-            pair = keep.tile([P, 2, P], F32, name=f"pair{lo}")
+        copies = (nc.scalar.copy, nc.vector.tensor_copy)
+        pairs = [
+            keep.tile([P, 2, P], F32, name="pair0"),
+            keep.tile([P, 2, P], F32, name="pair1"),
+        ]
+        for pair, lo in zip(pairs, (0, P)):
             for u in range(2):
                 copies[u](out=pair[:, u, :], in_=acc[u, lo][:])
             nc.sync.dma_start(first_rows[:, :, lo : lo + P], pair[:])
-        result = [keep.tile([P, V], F32, name=f"result{u}") for u in range(2)]
-        nc.vector.tensor_copy(out=result[0][:], in_=acc[2, 0][:])
-        nc.sync.dma_start(out[2 * P : 3 * P, :], result[0][:])
-        nc.scalar.copy(out=result[1][:, :P], in_=acc[3, 0][:])
-        nc.vector.tensor_copy(out=result[1][:, P:], in_=acc[3, P][:])
-        nc.sync.dma_start(out[3 * P :, :], result[1][:])
+        for u in range(2, 4):
+            result = keep.tile([P, V], F32, name=f"result{u}")
+            for copy, lo in zip(copies, (0, P)):
+                copy(out=result[:, lo : lo + P], in_=acc[u, lo][:])
+            nc.sync.dma_start(out[u * P : (u + 1) * P, :], result[:])

@@ -22,6 +22,8 @@ HALF = 256
 
 RUN = 4
 PLAIN = 2
+EARLY = 192
+QUARTER = 64
 
 
 def interleave(copy, grouped, raw, lo, hi, at=0):
@@ -54,7 +56,10 @@ def tile_picked_tokmixl_relu_p_kernel(tc, x_words, x_scales, wa, gt, w1, offs, f
             keep.tile([P, PACK, HALF], F32, name="wa_raw0", tag="wa_raw0", align_bytes=64),
             shared.tile([P, PACK, HALF], F32, name="wa_raw1", align_bytes=64, offset=0),
         ]
-        w1_raw = [late.tile([P, PACK, HALF], F32, name=f"w1_raw{h}", align_bytes=64, offset=4096 * h) for h in range(2)]
+        w1_raw = [
+            late.tile([P, PACK, EARLY], F32, name="w1_raw0", align_bytes=64, offset=1024),
+            late.tile([P, PACK, N - EARLY], F32, name="w1_raw1", align_bytes=64, offset=4096),
+        ]
 
         x_rows = x_words[0].rearrange("p n t -> p (n t)").bitcast(I32)
         wa_rows = wa.rearrange("(p t) c -> p t c", t=PACK)
@@ -82,13 +87,13 @@ def tile_picked_tokmixl_relu_p_kernel(tc, x_words, x_scales, wa, gt, w1, offs, f
         for r, queue in enumerate((nc.sync, nc.scalar, nc.sync, nc.scalar)):
             queue.dma_start(x_sc[r:P:32, :].bitcast(I32), picked_sc[8 * r : P : 32, :].bitcast(I32))
         gt_wide = keep.tile([P, PACK - PLAIN, V], F32, name="gt_wide", tag="wa_raw0", align_bytes=64)
-        nc.scalar.copy(out=gt_wide[:], in_=gt_sb[:, PLAIN:].unsqueeze(2).to_broadcast([P, PACK - PLAIN, V]))
+        nc.gpsimd.tensor_copy(out=gt_wide[:], in_=gt_sb[:, PLAIN:].unsqueeze(2).to_broadcast([P, PACK - PLAIN, V]))
 
         wa_codes = keep.tile([P, H], U32, name="wa_codes", tag="table_scales", align_bytes=64)
         quantize(nc, wa_codes, wa_sc, wa_lead, 0, P)
         quantize(nc, wa_codes, wa_sc, wa_grouped, P, HALF)
-        for h in range(2):
-            nc.sync.dma_start(w1_raw[h][:], w1_rows[:, :, h * HALF : (h + 1) * HALF])
+        nc.sync.dma_start(w1_raw[0][:], w1_rows[:, :, :EARLY])
+        nc.sync.dma_start(w1_raw[1][:], w1_rows[:, :, EARLY:])
         nc.vector.tensor_copy(
             x_codes[:].rearrange("p (t m) -> p m t", t=PACK), table_words[:].bitcast(U32).indirect(offs_sb[:])
         )
@@ -137,15 +142,28 @@ def tile_picked_tokmixl_relu_p_kernel(tc, x_words, x_scales, wa, gt, w1, offs, f
             )
 
         w1_grouped = [
-            shared.tile([P, PACK * HALF], BF16, name=f"w1_grouped{h}", align_bytes=64, offset=at)
-            for h, at in enumerate((4 * H * PACK, 4 * H))
+            shared.tile([P, width], BF16, name=f"w1_grouped{u}", align_bytes=64, offset=at)
+            for u, (at, width) in enumerate(((8192, 512), (9216, 512), (4096, 512), (12288, 1536)))
         ]
-        w1_codes = [keep.tile([P, HALF], U32, name=f"w1_codes{h}", align_bytes=64) for h in range(2)]
-        w1_sc = [keep.tile([P, HALF], U8, name=f"w1_sc{h}", align_bytes=64) for h in range(2)]
-        for lo in (0, P):
-            interleave(nc.vector.tensor_copy, w1_grouped[0], w1_raw[0], lo, lo + P)
-        for lo in (0, P):
-            quantize(nc, w1_codes[0], w1_sc[0], w1_grouped[0], lo, lo + P)
+        w1_codes = [
+            keep.tile([P, P], U32, name="w1_codes0", align_bytes=64),
+            keep.tile([P, P], U32, name="w1_codes1", align_bytes=64),
+            shared.tile([P, P], U32, name="w1_codes2", align_bytes=64, offset=16384),
+            shared.tile([P, P], U32, name="w1_codes3", align_bytes=64, offset=16384 + 512),
+        ]
+        w1_sc = [keep.tile([P, P], U8, name=f"w1_sc{u}", align_bytes=64) for u in range(4)]
+        interleave(nc.vector.tensor_copy, w1_grouped[0], w1_raw[0], 0, P)
+        interleave(nc.vector.tensor_copy, w1_grouped[1], w1_raw[0], P, EARLY, -P)
+        quantize(nc, w1_codes[0], w1_sc[0], w1_grouped[0], 0, P)
+        quantize(nc, w1_codes[1], w1_sc[1], w1_grouped[1], 0, QUARTER)
+        nc.gpsimd.tensor_scalar(
+            out=w1_grouped[3][:, : PACK * P].rearrange("p (c t) -> p c t", t=PACK),
+            in0=w1_raw[1][:, :, N - EARLY - P :].rearrange("p t c -> p c t"),
+            scalar1=1.0,
+            scalar2=0.0,
+            op0=ALU.mult,
+            op1=ALU.add,
+        )
 
         z = late.tile([P, PACK, V], F32, name="z", align_bytes=64, offset=0)
         for t in range(PLAIN):
@@ -157,46 +175,37 @@ def tile_picked_tokmixl_relu_p_kernel(tc, x_words, x_scales, wa, gt, w1, offs, f
                 )
         for t in range(PLAIN):
             nc.scalar.activation(out=z[:, t, :], in_=z[:, t, :], func=ACT.Copy, scale=gt_sb[:, t : t + 1])
-        for lo in (0, P):
-            interleave(nc.scalar.copy, w1_grouped[1], w1_raw[1], lo, lo + P)
+        w1_middle = shared.tile([P, PACK * QUARTER], BF16, name="w1_middle", align_bytes=64, offset=5120)
+        interleave(nc.scalar.copy, w1_grouped[2], w1_raw[1], QUARTER, QUARTER + P, -QUARTER)
+        interleave(nc.scalar.copy, w1_middle, w1_raw[1], 0, QUARTER)
 
         z_codes = keep.tile([P, V], U32, name="z_codes", align_bytes=64)
         z_sc = keep.tile([P, V], U8, name="z_sc", align_bytes=64)
-        z_grouped = keep.tile([P, PACK * V], BF16, name="z_grouped", tag="z_grouped", align_bytes=64)
+        z_grouped = shared.tile([P, PACK * V], BF16, name="z_grouped", align_bytes=64, offset=16384)
         for lo in (0, P):
             interleave(nc.vector.tensor_copy, z_grouped, z, lo, lo + P)
         for lo in (0, P):
             quantize(nc, z_codes, z_sc, z_grouped, lo, lo + P)
-        for lo in (0, P):
-            quantize(nc, w1_codes[1], w1_sc[1], w1_grouped[1], lo, lo + P)
+        nc.vector.quantize_mx(
+            out=w1_codes[1][:, QUARTER:].bitcast(FP8X4), scales=w1_sc[1][:, QUARTER:], in_=w1_middle[:]
+        )
+        for u in (2, 3):
+            quantize(nc, w1_codes[u], w1_sc[u], w1_grouped[u], 0, P)
 
-        banks = ((0, 0, P, 0), (1, 0, P, 2), (0, P, V, 1), (1, P, V, 3), (2, 0, P, 4), (2, P, V, 6), (3, 0, P, 5), (3, P, V, 7))
-        acc = {}
-        for u, lo, hi, bank in banks:
-            cols = slice((u % 2) * P, (u % 2 + 1) * P)
-            acc[u, lo] = psum.tile([P, hi - lo], F32, name=f"total{u}_{lo}", tag=f"bank{bank}")
-            for a in range(lo, hi, P):
+        copies = (nc.scalar.copy, nc.vector.tensor_copy)
+        banks = ((0, 1), (2, 3), (4, 5), (7, 6))
+        for u in range(4):
+            result = shared.tile([P, V], F32, name=f"result{u}", align_bytes=64, offset=12288 + 1024 * u)
+            for h, copy in enumerate(copies):
+                acc = psum.tile([P, P], F32, name=f"total{u}_{h}", tag=f"bank{banks[u][h]}")
                 nc.tensor.matmul_mx(
-                    out=acc[u, lo][:, a - lo : a - lo + P],
-                    lhsT=w1_codes[u // 2][:, cols].bitcast(FP8X4),
-                    lhsT_scale=w1_sc[u // 2][:, cols],
-                    rhs=z_codes[:, a : a + P].bitcast(FP8X4),
-                    rhs_scale=z_sc[:, a : a + P],
+                    out=acc[:],
+                    lhsT=w1_codes[u][:].bitcast(FP8X4),
+                    lhsT_scale=w1_sc[u][:],
+                    rhs=z_codes[:, h * P : (h + 1) * P].bitcast(FP8X4),
+                    rhs_scale=z_sc[:, h * P : (h + 1) * P],
                     start=True,
                     stop=True,
                 )
-        first_rows = out[: 2 * P, :].rearrange("(u p) v -> p u v", p=P)
-        copies = (nc.scalar.copy, nc.vector.tensor_copy)
-        pairs = [
-            keep.tile([P, 2, P], F32, name="pair0"),
-            keep.tile([P, 2, P], F32, name="pair1"),
-        ]
-        for pair, lo in zip(pairs, (0, P)):
-            for u in range(2):
-                copies[u](out=pair[:, u, :], in_=acc[u, lo][:])
-            nc.sync.dma_start(first_rows[:, :, lo : lo + P], pair[:])
-        for u in range(2, 4):
-            result = keep.tile([P, V], F32, name=f"result{u}")
-            for copy, lo in zip(copies, (0, P)):
-                copy(out=result[:, lo : lo + P], in_=acc[u, lo][:])
+                copy(out=result[:, h * P : (h + 1) * P], in_=acc[:])
             nc.sync.dma_start(out[u * P : (u + 1) * P, :], result[:])

@@ -22,8 +22,8 @@ HALF = 256
 
 RUN = 4
 PLAIN = 2
-EARLY = 192
-QUARTER = 64
+EARLY = 256
+STEP = 64
 
 
 def interleave(copy, grouped, raw, lo, hi, at=0):
@@ -57,7 +57,7 @@ def tile_picked_tokmixl_relu_p_kernel(tc, x_words, x_scales, wa, gt, w1, offs, f
             shared.tile([P, PACK, HALF], F32, name="wa_raw1", align_bytes=64, offset=0),
         ]
         w1_raw = [
-            late.tile([P, PACK, EARLY], F32, name="w1_raw0", align_bytes=64, offset=1024),
+            late.tile([P, PACK, EARLY], F32, name="w1_raw0", align_bytes=64, offset=0),
             late.tile([P, PACK, N - EARLY], F32, name="w1_raw1", align_bytes=64, offset=4096),
         ]
 
@@ -141,31 +141,36 @@ def tile_picked_tokmixl_relu_p_kernel(tc, x_words, x_scales, wa, gt, w1, offs, f
                 stop=True,
             )
 
-        w1_grouped = [
-            shared.tile([P, width], BF16, name=f"w1_grouped{u}", align_bytes=64, offset=at)
-            for u, (at, width) in enumerate(((8192, 512), (9216, 512), (4096, 512), (12288, 1536)))
+        w1_steps = [
+            shared.tile([P, PACK * STEP], BF16, name=f"w1_step{s}", align_bytes=64, offset=at)
+            for s, at in enumerate((11776, 12288))
         ]
+        w1_grouped = {
+            u: shared.tile([P, width], BF16, name=f"w1_grouped{u}", align_bytes=64, offset=at)
+            for u, at, width in ((1, 12288, 2048), (2, 4096, 512), (3, 5120, 512))
+        }
         w1_codes = [
             keep.tile([P, P], U32, name="w1_codes0", align_bytes=64),
-            keep.tile([P, P], U32, name="w1_codes1", align_bytes=64),
+            shared.tile([P, P], U32, name="w1_codes1", align_bytes=64, offset=16384 + 1024),
             shared.tile([P, P], U32, name="w1_codes2", align_bytes=64, offset=16384),
             shared.tile([P, P], U32, name="w1_codes3", align_bytes=64, offset=16384 + 512),
         ]
         w1_sc = [keep.tile([P, P], U8, name=f"w1_sc{u}", align_bytes=64) for u in range(4)]
-        interleave(nc.vector.tensor_copy, w1_grouped[0], w1_raw[0], 0, P)
-        interleave(nc.vector.tensor_copy, w1_grouped[1], w1_raw[0], P, EARLY, -P)
-        quantize(nc, w1_codes[0], w1_sc[0], w1_grouped[0], 0, P)
-        quantize(nc, w1_codes[1], w1_sc[1], w1_grouped[1], 0, QUARTER)
+        for s in range(2):
+            interleave(nc.vector.tensor_copy, w1_steps[s], w1_raw[0], s * STEP, (s + 1) * STEP, -s * STEP)
+        for s in range(2):
+            cols = slice(s * STEP, (s + 1) * STEP)
+            nc.vector.quantize_mx(out=w1_codes[0][:, cols].bitcast(FP8X4), scales=w1_sc[0][:, cols], in_=w1_steps[s][:])
         nc.gpsimd.tensor_scalar(
-            out=w1_grouped[3][:, : PACK * P].rearrange("p (c t) -> p c t", t=PACK),
-            in0=w1_raw[1][:, :, N - EARLY - P :].rearrange("p t c -> p c t"),
+            out=w1_grouped[1][:, : PACK * P].rearrange("p (c t) -> p c t", t=PACK),
+            in0=w1_raw[0][:, :, P:].rearrange("p t c -> p c t"),
             scalar1=1.0,
             scalar2=0.0,
             op0=ALU.mult,
             op1=ALU.add,
         )
 
-        z = late.tile([P, PACK, V], F32, name="z", align_bytes=64, offset=0)
+        z = shared.tile([P, PACK, V], F32, name="z", align_bytes=64, offset=8192)
         for t in range(PLAIN):
             nc.vector.tensor_copy(z[:, t, :], y[t][:].indirect(fl_sb[:]))
         for t in range(PLAIN, PACK):
@@ -175,28 +180,28 @@ def tile_picked_tokmixl_relu_p_kernel(tc, x_words, x_scales, wa, gt, w1, offs, f
                 )
         for t in range(PLAIN):
             nc.scalar.activation(out=z[:, t, :], in_=z[:, t, :], func=ACT.Copy, scale=gt_sb[:, t : t + 1])
-        w1_middle = shared.tile([P, PACK * QUARTER], BF16, name="w1_middle", align_bytes=64, offset=5120)
-        interleave(nc.scalar.copy, w1_grouped[2], w1_raw[1], QUARTER, QUARTER + P, -QUARTER)
-        interleave(nc.scalar.copy, w1_middle, w1_raw[1], 0, QUARTER)
+        for u in (2, 3):
+            interleave(nc.scalar.copy, w1_grouped[u], w1_raw[1], (u - 2) * P, (u - 1) * P, (2 - u) * P)
 
         z_codes = keep.tile([P, V], U32, name="z_codes", align_bytes=64)
         z_sc = keep.tile([P, V], U8, name="z_sc", align_bytes=64)
-        z_grouped = shared.tile([P, PACK * V], BF16, name="z_grouped", align_bytes=64, offset=16384)
-        for lo in (0, P):
-            interleave(nc.vector.tensor_copy, z_grouped, z, lo, lo + P)
-        for lo in (0, P):
-            quantize(nc, z_codes, z_sc, z_grouped, lo, lo + P)
-        nc.vector.quantize_mx(
-            out=w1_codes[1][:, QUARTER:].bitcast(FP8X4), scales=w1_sc[1][:, QUARTER:], in_=w1_middle[:]
-        )
-        for u in (2, 3):
+        z_grouped = [
+            shared.tile([P, PACK * P], BF16, name="z_grouped0", align_bytes=64, offset=16384 + 256),
+            keep.tile([P, PACK * P], BF16, name="z_grouped1", align_bytes=64),
+        ]
+        for h in range(2):
+            interleave(nc.vector.tensor_copy, z_grouped[h], z, h * P, (h + 1) * P, -h * P)
+        for h in range(2):
+            cols = slice(h * P, (h + 1) * P)
+            nc.vector.quantize_mx(out=z_codes[:, cols].bitcast(FP8X4), scales=z_sc[:, cols], in_=z_grouped[h][:])
+        for u in (2, 3, 1):
             quantize(nc, w1_codes[u], w1_sc[u], w1_grouped[u], 0, P)
 
         copies = (nc.scalar.copy, nc.vector.tensor_copy)
         banks = ((0, 1), (2, 3), (4, 5), (7, 6))
-        for u in range(4):
-            result = shared.tile([P, V], F32, name=f"result{u}", align_bytes=64, offset=12288 + 1024 * u)
-            for h, copy in enumerate(copies):
+        for u in (0, 2, 3, 1):
+            result = shared.tile([P, V], F32, name=f"result{u}", align_bytes=64, offset=12288 + 1024 * u if u else 18432)
+            for h, copy in enumerate(copies if u else (nc.scalar.copy, nc.scalar.copy)):
                 acc = psum.tile([P, P], F32, name=f"total{u}_{h}", tag=f"bank{banks[u][h]}")
                 nc.tensor.matmul_mx(
                     out=acc[:],

@@ -22,8 +22,9 @@ HALF = 256
 
 RUN = 4
 PLAIN = 2
-EARLY = 256
+EARLY = 192
 STEP = 64
+SHARE = 32
 
 
 def interleave(copy, grouped, raw, lo, hi, at=0):
@@ -58,7 +59,7 @@ def tile_picked_tokmixl_relu_p_kernel(tc, x_words, x_scales, wa, gt, w1, offs, f
         ]
         w1_raw = [
             late.tile([P, PACK, EARLY], F32, name="w1_raw0", align_bytes=64, offset=0),
-            late.tile([P, PACK, N - EARLY], F32, name="w1_raw1", align_bytes=64, offset=4096),
+            late.tile([P, PACK, N - EARLY], F32, name="w1_raw1", align_bytes=64, offset=3072),
         ]
 
         x_rows = x_words[0].rearrange("p n t -> p (n t)").bitcast(I32)
@@ -74,9 +75,8 @@ def tile_picked_tokmixl_relu_p_kernel(tc, x_words, x_scales, wa, gt, w1, offs, f
         nc.sync.dma_start(fl_sb[:], fl)
 
         wa_sc = keep.tile([P, H], U8, name="wa_sc", align_bytes=64)
-        wa_lead = late.tile([P, PACK * P], BF16, name="wa_lead", align_bytes=64, offset=3584)
+        wa_lead = late.tile([P, PACK * P], BF16, name="wa_lead", align_bytes=64, offset=2560)
         wa_grouped = shared.tile([P, PACK * H], BF16, name="wa_grouped", align_bytes=64, offset=4 * H * PACK)
-        wa_third = keep.tile([P, PACK * P], BF16, name="wa_third", tag="table_words", align_bytes=64)
         interleave(nc.scalar.copy, wa_lead, wa_raw[0], 0, P)
         interleave(nc.scalar.copy, wa_grouped, wa_raw[0], P, HALF)
 
@@ -97,37 +97,39 @@ def tile_picked_tokmixl_relu_p_kernel(tc, x_words, x_scales, wa, gt, w1, offs, f
         nc.vector.tensor_copy(
             x_codes[:].rearrange("p (t m) -> p m t", t=PACK), table_words[:].bitcast(U32).indirect(offs_sb[:])
         )
-        interleave(nc.scalar.copy, wa_grouped, wa_raw[1], P, HALF, HALF)
-        interleave(nc.vector.tensor_copy, wa_third, wa_raw[1], 0, P)
-        nc.vector.quantize_mx(
-            out=wa_codes[:, HALF : HALF + P].bitcast(FP8X4), scales=wa_sc[:, HALF : HALF + P], in_=wa_third[:]
-        )
+        interleave(nc.scalar.copy, wa_grouped, wa_raw[1], P + SHARE, HALF, HALF)
+        interleave(nc.vector.tensor_copy, wa_grouped, wa_raw[1], 0, P, HALF)
+        interleave(nc.vector.tensor_copy, wa_grouped, wa_raw[1], P, P + SHARE, HALF)
+        quantize(nc, wa_codes, wa_sc, wa_grouped, HALF, HALF + P)
         quantize(nc, wa_codes, wa_sc, wa_grouped, HALF + P, H)
 
         y = [shared.tile([P, H], F32, name=f"y{t}", align_bytes=64, offset=4 * H * t) for t in range(PACK)]
 
-        def project(t, lo, hi, bank, width=P):
+        def project(acc, t, lo, hi, at=0):
+            nc.tensor.matmul_mx(
+                out=acc[:, lo - at : hi - at],
+                lhsT=x_codes[:, t * P : (t + 1) * P].bitcast(FP8X4),
+                lhsT_scale=x_sc[:, t * P : (t + 1) * P],
+                rhs=wa_codes[:, lo:hi].bitcast(FP8X4),
+                rhs_scale=wa_sc[:, lo:hi],
+                start=True,
+                stop=True,
+            )
+
+        def piece(t, lo, hi, bank):
             acc = psum.tile([P, hi - lo], F32, name=f"acc{t}_{lo}", tag=f"bank{bank}")
-            for a in reversed(range(lo, hi, width)):
-                b = min(a + width, hi)
-                nc.tensor.matmul_mx(
-                    out=acc[:, a - lo : b - lo],
-                    lhsT=x_codes[:, t * P : (t + 1) * P].bitcast(FP8X4),
-                    lhsT_scale=x_sc[:, t * P : (t + 1) * P],
-                    rhs=wa_codes[:, a:b].bitcast(FP8X4),
-                    rhs_scale=wa_sc[:, a:b],
-                    start=True,
-                    stop=True,
-                )
+            project(acc, t, lo, hi, lo)
             nc.scalar.activation(out=y[t][:, lo:hi], in_=acc[:], func=ACT.Relu)
 
-        project(0, 0, HALF, 0, HALF)
-        project(1, 0, HALF, 1, HALF)
-        project(0, HALF, HALF + P, 2)
-        project(0, HALF + P, H, 3)
-        project(1, HALF, H, 4, HALF)
-        project(2, 0, H, 5, H)
-        project(3, 0, H, 6, H)
+        piece(0, 0, HALF, 0)
+        second = psum.tile([P, H], F32, name="second", tag="bank1")
+        project(second, 1, 0, HALF)
+        piece(0, HALF, HALF + P, 2)
+        piece(0, HALF + P, H, 3)
+        project(second, 1, HALF, H)
+        nc.scalar.activation(out=y[1][:], in_=second[:], func=ACT.Relu)
+        piece(2, 0, H, 5)
+        piece(3, 0, H, 6)
 
         for g in range(2):
             unread = psum.tile([32, H], F32, name=f"unread{g}", tag="bank6")
@@ -147,8 +149,9 @@ def tile_picked_tokmixl_relu_p_kernel(tc, x_words, x_scales, wa, gt, w1, offs, f
         ]
         w1_grouped = {
             u: shared.tile([P, width], BF16, name=f"w1_grouped{u}", align_bytes=64, offset=at)
-            for u, at, width in ((1, 12288, 2048), (2, 4096, 512), (3, 5120, 512))
+            for u, at, width in ((1, 12288, 2048), (2, 3584, 512), (3, 4608, 512))
         }
+        w1_middle = shared.tile([P, PACK * STEP], BF16, name="w1_middle", align_bytes=64, offset=5632)
         w1_codes = [
             keep.tile([P, P], U32, name="w1_codes0", align_bytes=64),
             shared.tile([P, P], U32, name="w1_codes1", align_bytes=64, offset=16384 + 1024),
@@ -162,7 +165,7 @@ def tile_picked_tokmixl_relu_p_kernel(tc, x_words, x_scales, wa, gt, w1, offs, f
             cols = slice(s * STEP, (s + 1) * STEP)
             nc.vector.quantize_mx(out=w1_codes[0][:, cols].bitcast(FP8X4), scales=w1_sc[0][:, cols], in_=w1_steps[s][:])
         nc.gpsimd.tensor_scalar(
-            out=w1_grouped[1][:, : PACK * P].rearrange("p (c t) -> p c t", t=PACK),
+            out=w1_grouped[1][:, : PACK * STEP].rearrange("p (c t) -> p c t", t=PACK),
             in0=w1_raw[0][:, :, P:].rearrange("p t c -> p c t"),
             scalar1=1.0,
             scalar2=0.0,
@@ -181,7 +184,8 @@ def tile_picked_tokmixl_relu_p_kernel(tc, x_words, x_scales, wa, gt, w1, offs, f
         for t in range(PLAIN):
             nc.scalar.activation(out=z[:, t, :], in_=z[:, t, :], func=ACT.Copy, scale=gt_sb[:, t : t + 1])
         for u in (2, 3):
-            interleave(nc.scalar.copy, w1_grouped[u], w1_raw[1], (u - 2) * P, (u - 1) * P, (2 - u) * P)
+            interleave(nc.scalar.copy, w1_grouped[u], w1_raw[1], u * P - EARLY, (u + 1) * P - EARLY, EARLY - u * P)
+        interleave(nc.scalar.copy, w1_middle, w1_raw[1], 0, STEP)
 
         z_codes = keep.tile([P, V], U32, name="z_codes", align_bytes=64)
         z_sc = keep.tile([P, V], U8, name="z_sc", align_bytes=64)
@@ -194,8 +198,10 @@ def tile_picked_tokmixl_relu_p_kernel(tc, x_words, x_scales, wa, gt, w1, offs, f
         for h in range(2):
             cols = slice(h * P, (h + 1) * P)
             nc.vector.quantize_mx(out=z_codes[:, cols].bitcast(FP8X4), scales=z_sc[:, cols], in_=z_grouped[h][:])
-        for u in (2, 3, 1):
+        for u in (2, 3):
             quantize(nc, w1_codes[u], w1_sc[u], w1_grouped[u], 0, P)
+        nc.vector.quantize_mx(out=w1_codes[1][:, STEP:].bitcast(FP8X4), scales=w1_sc[1][:, STEP:], in_=w1_middle[:])
+        quantize(nc, w1_codes[1], w1_sc[1], w1_grouped[1], 0, STEP)
 
         copies = (nc.scalar.copy, nc.vector.tensor_copy)
         banks = ((0, 1), (2, 3), (4, 5), (7, 6))

from contextlib import ExitStack

import concourse.mybir as mybir

K, T, S, V, N, H = 512, 2048, 512, 256, 512, 512
FLOPS = 2 * K * S * H + 2 * S * N * V

F32 = mybir.dt.float32
BF16 = mybir.dt.bfloat16
I32 = mybir.dt.int32
U32 = mybir.dt.uint32
U16 = mybir.dt.uint16
U8 = mybir.dt.uint8
FP8X4 = mybir.dt.float8_e4m3fn_x4
ALU = mybir.AluOpType
ACT = mybir.ActivationFunctionType

P = 128
PACK = 4
HALF = 256


RUN = 4
PLAIN = 2
EARLY = 192
STEP = 64
SHARE = 32


def interleave(copy, grouped, raw, lo, hi, at=0):
    copy(
        out=grouped[:, PACK * (at + lo) : PACK * (at + hi)].rearrange("p (c i t) -> p c t i", i=RUN, t=PACK),
        in_=raw[:, :, lo:hi].rearrange("p t (c i) -> p c t i", i=RUN),
    )


def quantize(nc, codes, scales, grouped, lo, hi):
    nc.vector.quantize_mx(
        out=codes[:, lo:hi].bitcast(FP8X4), scales=scales[:, lo:hi], in_=grouped[:, PACK * lo : PACK * hi]
    )


def tile_picked_tokmixl_relu_p_kernel(tc, x_words, x_scales, wa, gt, w1, offs, fl, out):
    nc = tc.nc
    with ExitStack() as ctx:
        keep = ctx.enter_context(tc.tile_pool(name="keep", bufs=1))
        shared = ctx.enter_context(tc.tile_pool(name="shared", bufs=1))
        late = ctx.enter_context(tc.tile_pool(name="late", bufs=1))
        psum = ctx.enter_context(tc.psum_pool(name="psum", bufs=1))

        offs_sb = keep.tile([P, S // 16], U16, name="offs_sb")
        fl_sb = keep.tile([P, V // 16], U16, name="fl_sb")
        table_words = keep.tile([P, T], I32, name="table_words", tag="table_words", align_bytes=64)
        table_scales = keep.tile([P, T], U8, name="table_scales", tag="table_scales", align_bytes=64)
        gt_sb = keep.tile([P, PACK], F32, name="gt_sb")
        wa_raw = [
            keep.tile([P, PACK, HALF], F32, name="wa_raw0", tag="wa_raw0", align_bytes=64),
            shared.tile([P, PACK, HALF], F32, name="wa_raw1", align_bytes=64, offset=0),
        ]
        w1_raw = [
            late.tile([P, PACK, EARLY], F32, name="w1_raw0", align_bytes=64, offset=0),
            late.tile([P, PACK, N - EARLY], F32, name="w1_raw1", align_bytes=64, offset=3072),
        ]

        x_rows = x_words[0].rearrange("p n t -> p (n t)").bitcast(I32)
        wa_rows = wa.rearrange("(p t) c -> p t c", t=PACK)
        w1_rows = w1.rearrange("(p t) c -> p t c", t=PACK)
        nc.gpsimd.dma_start(gt_sb[:], gt.rearrange("(p t) o -> p (t o)", t=PACK))
        nc.vector.memset(table_scales[:].bitcast(I32), 0)
        nc.sync.dma_start(wa_raw[0][:], wa_rows[:, :, :HALF])
        nc.sync.dma_start(offs_sb[:], offs)
        nc.sync.dma_start(table_scales[0:P:8, :].bitcast(I32), x_scales[0].bitcast(I32))
        nc.sync.dma_start(table_words[:], x_rows)
        nc.sync.dma_start(wa_raw[1][:], wa_rows[:, :, HALF:])
        nc.sync.dma_start(fl_sb[:], fl)

        wa_sc = keep.tile([P, H], U8, name="wa_sc", align_bytes=64)
        wa_lead = late.tile([P, PACK * P], BF16, name="wa_lead", align_bytes=64, offset=2560)
        wa_grouped = shared.tile([P, PACK * H], BF16, name="wa_grouped", align_bytes=64, offset=4 * H * PACK)
        interleave(nc.scalar.copy, wa_lead, wa_raw[0], 0, P)
        interleave(nc.scalar.copy, wa_grouped, wa_raw[0], P, HALF)

        picked_sc = keep.tile([P, S], U8, name="picked_sc", align_bytes=64)
        x_sc = keep.tile([P, S], U8, name="x_sc", align_bytes=64)
        x_codes = keep.tile([P, S], U32, name="x_codes", align_bytes=64)
        nc.vector.tensor_copy(picked_sc[:].rearrange("p (t m) -> p m t", t=PACK), table_scales[:].indirect(offs_sb[:]))
        for r, queue in enumerate((nc.sync, nc.scalar, nc.sync, nc.scalar)):
            queue.dma_start(x_sc[r:P:32, :].bitcast(I32), picked_sc[8 * r : P : 32, :].bitcast(I32))
        gt_wide = keep.tile([P, PACK - PLAIN, V], F32, name="gt_wide", tag="wa_raw0", align_bytes=64)
        nc.gpsimd.tensor_copy(out=gt_wide[:], in_=gt_sb[:, PLAIN:].unsqueeze(2).to_broadcast([P, PACK - PLAIN, V]))

        wa_codes = keep.tile([P, H], U32, name="wa_codes", tag="table_scales", align_bytes=64)
        quantize(nc, wa_codes, wa_sc, wa_lead, 0, P)
        quantize(nc, wa_codes, wa_sc, wa_grouped, P, HALF)
        nc.sync.dma_start(w1_raw[0][:], w1_rows[:, :, :EARLY])
        nc.sync.dma_start(w1_raw[1][:], w1_rows[:, :, EARLY:])
        nc.vector.tensor_copy(
            x_codes[:].rearrange("p (t m) -> p m t", t=PACK), table_words[:].bitcast(U32).indirect(offs_sb[:])
        )
        interleave(nc.scalar.copy, wa_grouped, wa_raw[1], P + SHARE, HALF, HALF)
        interleave(nc.vector.tensor_copy, wa_grouped, wa_raw[1], 0, P, HALF)
        interleave(nc.vector.tensor_copy, wa_grouped, wa_raw[1], P, P + SHARE, HALF)
        quantize(nc, wa_codes, wa_sc, wa_grouped, HALF, HALF + P)
        quantize(nc, wa_codes, wa_sc, wa_grouped, HALF + P, H)

        y = [shared.tile([P, H], F32, name=f"y{t}", align_bytes=64, offset=4 * H * t) for t in range(PACK)]

        def project(acc, t, lo, hi, at=0):
            nc.tensor.matmul_mx(
                out=acc[:, lo - at : hi - at],
                lhsT=x_codes[:, t * P : (t + 1) * P].bitcast(FP8X4),
                lhsT_scale=x_sc[:, t * P : (t + 1) * P],
                rhs=wa_codes[:, lo:hi].bitcast(FP8X4),
                rhs_scale=wa_sc[:, lo:hi],
                start=True,
                stop=True,
            )

        def piece(t, lo, hi, bank):
            acc = psum.tile([P, hi - lo], F32, name=f"acc{t}_{lo}", tag=f"bank{bank}")
            project(acc, t, lo, hi, lo)
            nc.scalar.activation(out=y[t][:, lo:hi], in_=acc[:], func=ACT.Relu)

        piece(0, 0, HALF, 0)
        second = psum.tile([P, H], F32, name="second", tag="bank1")
        project(second, 1, 0, HALF)
        piece(0, HALF, HALF + P, 2)
        piece(0, HALF + P, H, 3)
        project(second, 1, HALF, H)
        nc.scalar.activation(out=y[1][:], in_=second[:], func=ACT.Relu)
        piece(2, 0, H, 5)
        piece(3, 0, H, 6)

        for g in range(2):
            unread = psum.tile([32, H], F32, name=f"unread{g}", tag="bank6")
            nc.tensor.matmul_mx(
                out=unread[:],
                lhsT=wa_codes[:, g * 64 : g * 64 + 32].bitcast(FP8X4),
                lhsT_scale=wa_sc[:, g * 64 : g * 64 + 32],
                rhs=wa_codes[:].bitcast(FP8X4),
                rhs_scale=wa_sc[:],
                start=True,
                stop=True,
            )

        w1_steps = [
            shared.tile([P, PACK * STEP], BF16, name=f"w1_step{s}", align_bytes=64, offset=at)
            for s, at in enumerate((11776, 12288))
        ]
        w1_grouped = {
            u: shared.tile([P, width], BF16, name=f"w1_grouped{u}", align_bytes=64, offset=at)
            for u, at, width in ((1, 12288, 2048), (2, 3584, 512), (3, 4608, 512))
        }
        w1_middle = shared.tile([P, PACK * STEP], BF16, name="w1_middle", align_bytes=64, offset=5632)
        w1_codes = [
            keep.tile([P, P], U32, name="w1_codes0", align_bytes=64),
            shared.tile([P, P], U32, name="w1_codes1", align_bytes=64, offset=16384 + 1024),
            shared.tile([P, P], U32, name="w1_codes2", align_bytes=64, offset=16384),
            shared.tile([P, P], U32, name="w1_codes3", align_bytes=64, offset=16384 + 512),
        ]
        w1_sc = [keep.tile([P, P], U8, name=f"w1_sc{u}", align_bytes=64) for u in range(4)]
        for s in range(2):
            interleave(nc.vector.tensor_copy, w1_steps[s], w1_raw[0], s * STEP, (s + 1) * STEP, -s * STEP)
        for s in range(2):
            cols = slice(s * STEP, (s + 1) * STEP)
            nc.vector.quantize_mx(out=w1_codes[0][:, cols].bitcast(FP8X4), scales=w1_sc[0][:, cols], in_=w1_steps[s][:])
        nc.gpsimd.tensor_scalar(
            out=w1_grouped[1][:, : PACK * STEP].rearrange("p (c t) -> p c t", t=PACK),
            in0=w1_raw[0][:, :, P:].rearrange("p t c -> p c t"),
            scalar1=1.0,
            scalar2=0.0,
            op0=ALU.mult,
            op1=ALU.add,
        )

        z = shared.tile([P, PACK, V], F32, name="z", align_bytes=64, offset=8192)
        for t in range(PLAIN):
            nc.vector.tensor_copy(z[:, t, :], y[t][:].indirect(fl_sb[:]))
        for t in range(PLAIN, PACK):
            for lo, hi in ((0, V),) if t < PACK - 1 else ((0, P), (P, V)):
                nc.vector.tensor_tensor(
                    z[:, t, lo:hi], y[t][:].indirect(fl_sb[:, lo // 16 : hi // 16]), gt_wide[:, t - PLAIN, lo:hi], ALU.mult
                )
        for t in range(PLAIN):
            nc.scalar.activation(out=z[:, t, :], in_=z[:, t, :], func=ACT.Copy, scale=gt_sb[:, t : t + 1])
        for u in (2, 3):
            interleave(nc.scalar.copy, w1_grouped[u], w1_raw[1], u * P - EARLY, (u + 1) * P - EARLY, EARLY - u * P)
        interleave(nc.scalar.copy, w1_middle, w1_raw[1], 0, STEP)

        z_codes = keep.tile([P, V], U32, name="z_codes", align_bytes=64)
        z_sc = keep.tile([P, V], U8, name="z_sc", align_bytes=64)
        z_grouped = [
            shared.tile([P, PACK * P], BF16, name="z_grouped0", align_bytes=64, offset=16384 + 256),
            keep.tile([P, PACK * P], BF16, name="z_grouped1", align_bytes=64),
        ]
        for h in range(2):
            interleave(nc.vector.tensor_copy, z_grouped[h], z, h * P, (h + 1) * P, -h * P)
        for h in range(2):
            cols = slice(h * P, (h + 1) * P)
            nc.vector.quantize_mx(out=z_codes[:, cols].bitcast(FP8X4), scales=z_sc[:, cols], in_=z_grouped[h][:])
        for u in (2, 3):
            quantize(nc, w1_codes[u], w1_sc[u], w1_grouped[u], 0, P)
        nc.vector.quantize_mx(out=w1_codes[1][:, STEP:].bitcast(FP8X4), scales=w1_sc[1][:, STEP:], in_=w1_middle[:])
        quantize(nc, w1_codes[1], w1_sc[1], w1_grouped[1], 0, STEP)

        copies = (nc.scalar.copy, nc.vector.tensor_copy)
        banks = ((0, 1), (2, 3), (4, 5), (7, 6))
        for u in (0, 2, 3, 1):
            result = shared.tile([P, V], F32, name=f"result{u}", align_bytes=64, offset=12288 + 1024 * u if u else 18432)
            for h, copy in enumerate(copies if u else (nc.scalar.copy, nc.scalar.copy)):
                acc = psum.tile([P, P], F32, name=f"total{u}_{h}", tag=f"bank{banks[u][h]}")
                nc.tensor.matmul_mx(
                    out=acc[:],
                    lhsT=w1_codes[u][:].bitcast(FP8X4),
                    lhsT_scale=w1_sc[u][:],
                    rhs=z_codes[:, h * P : (h + 1) * P].bitcast(FP8X4),
                    rhs_scale=z_sc[:, h * P : (h + 1) * P],
                    start=True,
                    stop=True,
                )
                copy(out=result[:, h * P : (h + 1) * P], in_=acc[:])
            nc.sync.dma_start(out[u * P : (u + 1) * P, :], result[:])
